import numpy as np
import ml_dtypes


def mxq(x, axis, fmt="e4m3"):
    dtype, down = {"e4m3": (ml_dtypes.float8_e4m3fn, 7), "e5m2": (ml_dtypes.float8_e5m2, 14)}[fmt]
    v = np.moveaxis(np.asarray(x, np.float32).astype(ml_dtypes.bfloat16).astype(np.float64), axis, -1)
    blocks = v.reshape(v.shape[:-1] + (-1, 32))
    amax = np.abs(blocks).max(-1, keepdims=True)
    byte = np.maximum(np.where(amax > 0, np.frexp(amax)[1] - 1 + 127, 0) - down, 1)
    scale = np.exp2(byte - 127.0)
    codes = (blocks / scale).astype(np.float32).astype(dtype).astype(np.float64)
    return np.moveaxis((codes * scale).reshape(v.shape), -1, axis)


WIDE = False


def mx_kscale(k):
    if not WIDE:
        return np.ones(k)
    levels = np.array([10, -10, 5, -5, 0])
    if k % 512:
        return np.exp2(np.random.permutation(np.resize(levels, k // 32))).repeat(32)
    a = np.empty((k // 512, 16))
    for p in range(k // 512):
        a[p, :8] = np.random.permutation(np.resize(levels, 8))
        for g in range(8):
            far = levels[np.abs(levels - a[p, g]) >= 10]
            a[p, g + 8] = far[np.random.randint(len(far))]
    return np.exp2(a.ravel()).repeat(32)


def f64(x):
    return np.asarray(x).astype(np.float64)


def striped(idx):
    return np.tile(np.asarray(idx).reshape(-1, 16).T, (8, 1)).astype(np.uint16)


def unstriped(offs):
    return offs[:16].T.reshape(-1).astype(np.int64)


E2M1 = np.array([0.0, 0.5, 1.0, 1.5, 2.0, 3.0, 4.0, 6.0, -0.0, -0.5, -1.0, -1.5, -2.0, -3.0, -4.0, -6.0])


def pack_weight(w, fmt):
    k, n = w.shape
    w = f64(np.asarray(w, np.float32).astype(ml_dtypes.bfloat16)).reshape(k // 32, 32, n)
    amax = np.abs(w).max(1)
    if fmt == "e4m3":
        byte = np.frexp(amax)[1] - 1 + 127 - 7
    else:
        mant, ex = np.frexp(amax / 6.0)
        byte = np.where(mant > 0.5, ex, ex - 1) + 127
    byte = np.clip(np.where(amax > 0, byte, 1), 1, 254)
    scaled = (w * np.exp2(127.0 - byte)[:, None, :]).reshape(k, n).astype(np.float32)
    by_word = np.ascontiguousarray(scaled.reshape(k // 512, 128, 4, n).transpose(0, 1, 3, 2))
    if fmt == "e4m3":
        words = by_word.astype(ml_dtypes.float8_e4m3fn).view(np.uint8)
    else:
        c = by_word.astype(ml_dtypes.float4_e2m1fn).view(np.uint8) & 0xF
        words = (c[..., 0::2] | (c[..., 1::2] << 4)).reshape(k // 512, 128, 2 * n)
    return np.ascontiguousarray(words), np.ascontiguousarray(byte.astype(np.uint8).reshape(k // 512, 16, n))


def unpack_weight(words, scales, fmt):
    g, _, n = scales.shape
    words = np.ascontiguousarray(words).reshape(g, 128, n, -1)
    if fmt == "e4m3":
        vals = words.view(ml_dtypes.float8_e4m3fn).astype(np.float64)
    else:
        nib = np.empty((g, 128, n, 4), np.uint8)
        nib[..., 0::2] = words & 0xF
        nib[..., 1::2] = words >> 4
        vals = E2M1[nib]
    vals = vals * np.repeat(np.exp2(scales.astype(np.float64) - 127.0), 8, axis=1)[..., None]
    return vals.transpose(0, 1, 3, 2).reshape(g * 512, n)


B, N, T, D, DV, NQ = 1, 2048, 4096, 512, 128, 128
PAGE = 512
CAP = 2.0


def setup_inputs():
    n = np.random.standard_normal
    pages = np.random.permutation(T // PAGE)[:B * N // PAGE]
    idx = (pages[:, None] * PAGE + np.arange(PAGE)[None, :]).reshape(-1)
    s = mx_kscale(D)[:, None]
    u = np.ones(T)
    u[idx] = mx_kscale(B * N)
    r = np.random.uniform(0.5, 2.0, T)
    k = n((D, T)) / s
    v = n((DV, T)) / (u * r)
    kp = pack_weight(k, "e4m3")
    vp = pack_weight(v.T, "e4m3")
    return {
        "qT": (n((B, D, NQ)) * s * (1.30 / np.sqrt(D))).astype(np.float32),
        "k_words": kp[0],
        "k_scales": kp[1],
        "v_words": vp[0],
        "v_scales": vp[1],
        "vs": np.tile(u * r, (128, 1)).astype(np.float32),
        "offs": striped(idx),
        "voffs": striped((pages[:, None] * DV + np.arange(DV)[None, :]).reshape(-1)),
    }


def reference(qT, k_words, k_scales, v_words, v_scales, vs, offs, voffs):
    idx = unstriped(offs)
    k = unpack_weight(k_words, k_scales, "e4m3")
    v = unpack_weight(v_words, v_scales, "e4m3")
    v = v.reshape(T // 512, 512, DV)[unstriped(voffs)[::DV] // DV].reshape(B, N, DV)
    pick = lambda x: x[:, idx].reshape(x.shape[0], B, N).transpose(1, 0, 2)
    q = f64(qT)
    score = mxq(q, 1, "e4m3").transpose(0, 2, 1) @ pick(k)
    score = CAP * np.tanh(score / CAP)
    m = score.max(-1, keepdims=True)
    p = np.exp(score - m)
    total = p.sum(-1, keepdims=True)
    w = p * pick(f64(vs))[:, :1, :]
    y = mxq(w, 2, "e4m3") @ v
    y = y / total
    return y

@@ -1,0 +1,176 @@
+from contextlib import ExitStack
+
+import concourse.mybir as mybir
+from concourse.masks import make_identity
+
+N, T, D, DV, NQ = 2048, 4096, 512, 128, 128
+PAGE = 512
+CAP = 2.0
+
+FLOPS = 2 * NQ * N * (D + DV)
+BYTES = D * NQ * 4 + D * T + 16 * T + T * DV + T // 32 * DV + T * 4 + 128 * (N + N // 4) // 16 * 2 + NQ * DV * 4
+
+F32 = mybir.dt.float32
+BF16 = mybir.dt.bfloat16
+I32 = mybir.dt.int32
+U32 = mybir.dt.uint32
+U16 = mybir.dt.uint16
+U8 = mybir.dt.uint8
+FP8X4 = mybir.dt.float8_e4m3fn_x4
+ALU = mybir.AluOpType
+ACT = mybir.ActivationFunctionType
+
+P = 128
+PACK = 4
+PAGES = N // PAGE
+POOL_PAGES = T // PAGE
+VS_ROW = 8
+
+
+def tile_attend_pkv8_cap_kernel(tc, qT, k_words, k_scales, v_words, v_scales, vs, offs, voffs, out):
+    nc = tc.nc
+    with ExitStack() as ctx:
+        sb = ctx.enter_context(tc.tile_pool(name="sb", bufs=1))
+        ps = ctx.enter_context(tc.psum_pool(name="ps", bufs=1))
+
+        offs_sb = sb.tile([P, N // 16], U16, name="offs_sb")
+        voffs_sb = sb.tile([P, PAGES * DV // 16], U16, name="voffs_sb")
+        k_pool = sb.tile([P, T], I32, name="k_pool", align_bytes=64)
+        ks_pool = sb.tile([P, T // 4], I32, name="ks_pool", align_bytes=64)
+        v_pool = sb.tile([P, POOL_PAGES * DV], I32, name="v_pool", align_bytes=64)
+        vsc_pool = sb.tile([P, POOL_PAGES * DV // 4], I32, name="vsc_pool", align_bytes=64)
+        vs_pool = sb.tile([P, T], F32, name="vs_pool", align_bytes=64)
+        q_raw = sb.tile([P, PACK, NQ], F32, name="q_raw")
+        ident = sb.tile([P, P], F32, name="ident")
+        warm = sb.tile([P, 1], F32, name="warm")
+
+        nc.vector.memset(ks_pool[:], 0)
+        nc.vector.memset(vs_pool[:], 0.0)
+        nc.vector.memset(vsc_pool[:], 0)
+        make_identity(nc, ident[:])
+        nc.scalar.activation(warm[:], ident[:, 0:1], ACT.Exp)
+
+        nc.sync.dma_start(offs_sb[:], offs)
+        nc.sync.dma_start(q_raw[:], qT[0].rearrange("(p j) q -> p j q", j=PACK))
+        for g in range(4):
+            nc.sync.dma_start(ks_pool[32 * g : 32 * g + 4, :], k_scales[0, 4 * g : 4 * g + 4, :].bitcast(I32))
+        nc.sync.dma_start(k_pool[:], k_words[0].rearrange("p t r -> p (t r)").bitcast(I32))
+        nc.scalar.dma_start(vs_pool[VS_ROW : VS_ROW + 1, :], vs[0:1, :])
+        nc.sync.dma_start(voffs_sb[:], voffs)
+        for g in range(4):
+            nc.sync.dma_start(
+                vsc_pool[32 * g : 32 * g + 4, :].rearrange("f (u e) -> f u e", u=POOL_PAGES),
+                v_scales[:, 4 * g : 4 * g + 4, :].bitcast(I32).rearrange("u f e -> f u e"),
+            )
+        nc.sync.dma_start(
+            v_pool[:].rearrange("p (u e) -> p u e", u=POOL_PAGES),
+            v_words.rearrange("u p e r -> p u (e r)").bitcast(I32),
+        )
+
+        q_bf = sb.tile([P, NQ, PACK], BF16, name="q_bf", align_bytes=64)
+        q_codes = sb.tile([P, NQ], U32, name="q_codes", align_bytes=64)
+        q_scales = sb.tile([P, NQ], U8, name="q_scales", align_bytes=64)
+        nc.scalar.copy(q_bf[:], q_raw[:].rearrange("p j q -> p q j"))
+
+        ks_g = sb.tile([P, N], U8, name="ks_g", align_bytes=64)
+        nc.vector.tensor_copy(ks_g[:], ks_pool[:].bitcast(U8).indirect(offs_sb[:]))
+        nc.vector.quantize_mx(out=q_codes[:].bitcast(FP8X4), scales=q_scales[:], in_=q_bf[:].rearrange("p q j -> p (q j)"))
+        vs_g = sb.tile([P, N], F32, name="vs_g", align_bytes=64)
+        nc.vector.tensor_copy(vs_g[:], vs_pool[:].indirect(offs_sb[:]))
+
+        vs_t = [sb.tile([P, 1, PACK], F32, name=f"vs_t{e}") for e in range(PAGES)]
+        for e in range(PAGES):
+            nc.sync.dma_start(
+                vs_t[e][:, 0, :],
+                vs_g[VS_ROW : VS_ROW + 1, e * PAGE : (e + 1) * PAGE].rearrange("o (p t) -> o p t", t=PACK),
+            )
+
+        k_g = sb.tile([P, N], U32, name="k_g", align_bytes=64)
+        th = sb.tile([P, PAGES, PACK, P], F32, name="th")
+        for e in range(PAGES):
+            cols = slice(e * PAGE, (e + 1) * PAGE)
+            nc.vector.tensor_copy(
+                k_g[:, cols], k_pool[:].bitcast(U32).indirect(offs_sb[:, e * PAGE // 16 : (e + 1) * PAGE // 16])
+            )
+            score = ps.tile([P, PAGE], F32, name=f"score{e}")
+            nc.tensor.matmul_mx(
+                out=score[:],
+                lhsT=q_codes[:].bitcast(FP8X4),
+                lhsT_scale=q_scales[:],
+                rhs=k_g[:, cols].bitcast(FP8X4),
+                rhs_scale=ks_g[:, cols],
+                start=True,
+                stop=True,
+            )
+            nc.scalar.activation(
+                th[:, e], score[:].rearrange("q (p t) -> q t p", t=PACK), ACT.Tanh, scale=1.0 / CAP
+            )
+
+        neg_c = sb.tile([P, PAGES, PACK, P], F32, name="neg_c")
+        neg_m_half = sb.tile([P, 1], F32, name="neg_m_half")
+        neg_m = sb.tile([P, 1], F32, name="neg_m")
+        flat = "q e t p -> q (e t p)"
+        nc.vector.tensor_scalar(
+            neg_c[:, 0:2].rearrange(flat), th[:, 0:2].rearrange(flat), -CAP, None, ALU.mult, ALU.min,
+            accum_out=neg_m_half[:],
+        )
+        nc.vector.tensor_scalar(
+            neg_c[:, 2:4].rearrange(flat), th[:, 2:4].rearrange(flat), -CAP, neg_m_half[:], ALU.mult, ALU.min,
+            accum_out=neg_m[:],
+        )
+
+        v_g = sb.tile([P, PAGES * DV], U32, name="v_g", align_bytes=64)
+        vsc_g = sb.tile([P, PAGES * DV], U8, name="vsc_g", align_bytes=64)
+        nc.vector.tensor_copy(v_g[:], v_pool[:].bitcast(U32).indirect(voffs_sb[:]))
+        nc.vector.tensor_copy(vsc_g[:], vsc_pool[:].bitcast(U8).indirect(voffs_sb[:]))
+
+        prob = sb.tile([P, PAGES, PACK, P], F32, name="prob")
+        l_page = sb.tile([P, PAGES], F32, name="l_page")
+        w_bf = [sb.tile([P, NQ, PACK], BF16, name=f"w_bf{e}", align_bytes=64) for e in range(PAGES)]
+        w_codes = [sb.tile([P, NQ], U32, name=f"w_codes{e}", align_bytes=64) for e in range(PAGES)]
+        w_scales = [sb.tile([P, NQ], U8, name=f"w_scales{e}", align_bytes=64) for e in range(PAGES)]
+
+        def quantize_page(e):
+            nc.vector.quantize_mx(
+                out=w_codes[e][:].bitcast(FP8X4), scales=w_scales[e][:], in_=w_bf[e][:].rearrange("p q t -> p (q t)")
+            )
+
+        for e in range(PAGES):
+            nc.scalar.activation(
+                prob[:, e].rearrange("q t p -> q (t p)"), neg_c[:, e].rearrange("q t p -> q (t p)"), ACT.Exp,
+                bias=neg_m[:], scale=-1.0, accum_out=l_page[:, e : e + 1],
+            )
+            turned = ps.tile([P, PACK, NQ], F32, name=f"turned{e}", tag=f"turned{e % 3}")
+            for t in range(PACK):
+                nc.tensor.transpose(turned[:, t, :], prob[:, e, t, :], ident[:])
+            nc.vector.tensor_tensor(
+                w_bf[e][:],
+                turned[:].rearrange("p t q -> p q t"),
+                vs_t[e][:].to_broadcast([P, NQ, PACK]),
+                ALU.mult,
+            )
+            if e > 0:
+                quantize_page(e - 1)
+        quantize_page(PAGES - 1)
+
+        l_copy = sb.tile([P, PAGES], F32, name="l_copy")
+        l_sum = sb.tile([P, 1], F32, name="l_sum")
+        l_inv = sb.tile([P, 1], F32, name="l_inv")
+        nc.scalar.activation(l_copy[:], l_page[:], ACT.Copy, accum_out=l_sum[:])
+        nc.vector.reciprocal(l_inv[:], l_sum[:])
+
+        acc = ps.tile([P, DV], F32, name="acc")
+        for e in range(PAGES):
+            cols = slice(e * DV, (e + 1) * DV)
+            nc.tensor.matmul_mx(
+                out=acc[:],
+                lhsT=w_codes[e][:].bitcast(FP8X4),
+                lhsT_scale=w_scales[e][:],
+                rhs=v_g[:, cols].bitcast(FP8X4),
+                rhs_scale=vsc_g[:, cols],
+                start=(e == 0),
+                stop=(e == PAGES - 1),
+            )
+        y = sb.tile([P, DV], F32, name="y")
+        nc.scalar.activation(y[:], acc[:], ACT.Copy, scale=l_inv[:])
+        nc.sync.dma_start(out[0], y[:])

@@ -1,7 +1,6 @@
 from contextlib import ExitStack
 
 import concourse.mybir as mybir
-from concourse.masks import make_identity
 
 N, T, D, DV, NQ = 2048, 4096, 512, 128, 128
 PAGE = 512
@@ -31,30 +30,37 @@ def tile_attend_pkv8_cap_kernel(tc, qT, k_words, k_scales, v_words, v_scales, vs
     nc = tc.nc
     with ExitStack() as ctx:
         sb = ctx.enter_context(tc.tile_pool(name="sb", bufs=1))
+        late = ctx.enter_context(tc.tile_pool(name="late", bufs=1))
         ps = ctx.enter_context(tc.psum_pool(name="ps", bufs=1))
 
         offs_sb = sb.tile([P, N // 16], U16, name="offs_sb")
         voffs_sb = sb.tile([P, PAGES * DV // 16], U16, name="voffs_sb")
-        k_pool = sb.tile([P, T], I32, name="k_pool", align_bytes=64)
+        diag = sb.tile([P, P], I32, name="diag", tag="k_slot", align_bytes=64)
         ks_pool = sb.tile([P, T // 4], I32, name="ks_pool", align_bytes=64)
-        v_pool = sb.tile([P, POOL_PAGES * DV], I32, name="v_pool", align_bytes=64)
         vsc_pool = sb.tile([P, POOL_PAGES * DV // 4], I32, name="vsc_pool", align_bytes=64)
         vs_pool = sb.tile([P, T], F32, name="vs_pool", align_bytes=64)
-        q_raw = sb.tile([P, PACK, NQ], F32, name="q_raw")
+        q_raw = sb.tile([P, PACK, NQ], F32, name="q_raw", tag="v_slot", align_bytes=64)
         ident = sb.tile([P, P], F32, name="ident")
         warm = sb.tile([P, 1], F32, name="warm")
 
+        nc.gpsimd.iota(diag[:], [[1, P]], base=0, channel_multiplier=-1)
         nc.vector.memset(ks_pool[:], 0)
+        nc.vector.tensor_scalar(ident[:], diag[:], 0.0, None, ALU.is_equal)
         nc.vector.memset(vs_pool[:], 0.0)
         nc.vector.memset(vsc_pool[:], 0)
-        make_identity(nc, ident[:])
         nc.scalar.activation(warm[:], ident[:, 0:1], ACT.Exp)
 
         nc.sync.dma_start(offs_sb[:], offs)
         nc.sync.dma_start(q_raw[:], qT[0].rearrange("(p j) q -> p j q", j=PACK))
         for g in range(4):
             nc.sync.dma_start(ks_pool[32 * g : 32 * g + 4, :], k_scales[0, 4 * g : 4 * g + 4, :].bitcast(I32))
+        k_pool = sb.tile([P, T], I32, name="k_pool", tag="k_slot", align_bytes=64)
         nc.sync.dma_start(k_pool[:], k_words[0].rearrange("p t r -> p (t r)").bitcast(I32))
+        q_bf = sb.tile([P, NQ, PACK], BF16, name="q_bf", align_bytes=64)
+        q_codes = sb.tile([P, NQ], U32, name="q_codes", align_bytes=64)
+        q_scales = sb.tile([P, NQ], U8, name="q_scales", align_bytes=64)
+        nc.scalar.copy(q_bf[:], q_raw[:].rearrange("p j q -> p q j"))
+
         nc.scalar.dma_start(vs_pool[VS_ROW : VS_ROW + 1, :], vs[0:1, :])
         nc.sync.dma_start(voffs_sb[:], voffs)
         for g in range(4):
@@ -62,70 +68,77 @@ def tile_attend_pkv8_cap_kernel(tc, qT, k_words, k_scales, v_words, v_scales, vs
                 vsc_pool[32 * g : 32 * g + 4, :].rearrange("f (u e) -> f u e", u=POOL_PAGES),
                 v_scales[:, 4 * g : 4 * g + 4, :].bitcast(I32).rearrange("u f e -> f u e"),
             )
+        v_pool = sb.tile([P, POOL_PAGES * DV], I32, name="v_pool", tag="v_slot", align_bytes=64)
         nc.sync.dma_start(
             v_pool[:].rearrange("p (u e) -> p u e", u=POOL_PAGES),
             v_words.rearrange("u p e r -> p u (e r)").bitcast(I32),
         )
 
-        q_bf = sb.tile([P, NQ, PACK], BF16, name="q_bf", align_bytes=64)
-        q_codes = sb.tile([P, NQ], U32, name="q_codes", align_bytes=64)
-        q_scales = sb.tile([P, NQ], U8, name="q_scales", align_bytes=64)
-        nc.scalar.copy(q_bf[:], q_raw[:].rearrange("p j q -> p q j"))
-
         ks_g = sb.tile([P, N], U8, name="ks_g", align_bytes=64)
         nc.vector.tensor_copy(ks_g[:], ks_pool[:].bitcast(U8).indirect(offs_sb[:]))
         nc.vector.quantize_mx(out=q_codes[:].bitcast(FP8X4), scales=q_scales[:], in_=q_bf[:].rearrange("p q j -> p (q j)"))
-        vs_g = sb.tile([P, N], F32, name="vs_g", align_bytes=64)
-        nc.vector.tensor_copy(vs_g[:], vs_pool[:].indirect(offs_sb[:]))
 
         vs_t = [sb.tile([P, 1, PACK], F32, name=f"vs_t{e}") for e in range(PAGES)]
-        for e in range(PAGES):
+
+        def page_offsets(e):
+            return offs_sb[:, e * PAGE // 16 : (e + 1) * PAGE // 16]
+
+        def gather_token_scales(e, tag):
+            vs_g = sb.tile([P, PAGE], F32, name=f"vs_g{e}", tag=tag, align_bytes=64)
+            nc.vector.tensor_copy(vs_g[:], vs_pool[:].indirect(page_offsets(e)))
             nc.sync.dma_start(
-                vs_t[e][:, 0, :],
-                vs_g[VS_ROW : VS_ROW + 1, e * PAGE : (e + 1) * PAGE].rearrange("o (p t) -> o p t", t=PACK),
+                vs_t[e][:, 0, :], vs_g[VS_ROW : VS_ROW + 1, :].rearrange("o (p t) -> o p t", t=PACK)
             )
 
-        k_g = sb.tile([P, N], U32, name="k_g", align_bytes=64)
-        th = sb.tile([P, PAGES, PACK, P], F32, name="th")
+        gather_token_scales(0, "vs_g0")
+        gather_token_scales(1, "vs_g1")
+
+        k_g = [sb.tile([P, PAGE], U32, name=f"k_g{e}", tag=f"k_g{e}", align_bytes=64) for e in range(PAGES)]
+        th_lo = sb.tile([P, 2, PACK, P], F32, name="th_lo")
+        th_hi = late.tile([P, 2, PACK, P], F32, name="th_hi", offset=0, align_bytes=64)
+        th = [th_lo[:, 0], th_lo[:, 1], th_hi[:, 0], th_hi[:, 1]]
         for e in range(PAGES):
             cols = slice(e * PAGE, (e + 1) * PAGE)
             nc.vector.tensor_copy(
-                k_g[:, cols], k_pool[:].bitcast(U32).indirect(offs_sb[:, e * PAGE // 16 : (e + 1) * PAGE // 16])
+                k_g[e][:], k_pool[:].bitcast(U32).indirect(page_offsets(e))
             )
-            score = ps.tile([P, PAGE], F32, name=f"score{e}")
+            score = ps.tile([P, PAGE], F32, name=f"score{e}", tag=f"bank{e}")
             nc.tensor.matmul_mx(
                 out=score[:],
                 lhsT=q_codes[:].bitcast(FP8X4),
                 lhsT_scale=q_scales[:],
-                rhs=k_g[:, cols].bitcast(FP8X4),
+                rhs=k_g[e][:].bitcast(FP8X4),
                 rhs_scale=ks_g[:, cols],
                 start=True,
                 stop=True,
             )
             nc.scalar.activation(
-                th[:, e], score[:].rearrange("q (p t) -> q t p", t=PACK), ACT.Tanh, scale=1.0 / CAP
+                th[e], score[:].rearrange("q (p t) -> q t p", t=PACK), ACT.Tanh, scale=1.0 / CAP
             )
+
+        gather_token_scales(2, "k_g0")
+        gather_token_scales(3, "k_g1")
 
         neg_c = sb.tile([P, PAGES, PACK, P], F32, name="neg_c")
         neg_m_half = sb.tile([P, 1], F32, name="neg_m_half")
         neg_m = sb.tile([P, 1], F32, name="neg_m")
         flat = "q e t p -> q (e t p)"
         nc.vector.tensor_scalar(
-            neg_c[:, 0:2].rearrange(flat), th[:, 0:2].rearrange(flat), -CAP, None, ALU.mult, ALU.min,
+            neg_c[:, 0:2].rearrange(flat), th_lo[:].rearrange(flat), -CAP, None, ALU.mult, ALU.min,
             accum_out=neg_m_half[:],
         )
         nc.vector.tensor_scalar(
-            neg_c[:, 2:4].rearrange(flat), th[:, 2:4].rearrange(flat), -CAP, neg_m_half[:], ALU.mult, ALU.min,
+            neg_c[:, 2:4].rearrange(flat), th_hi[:].rearrange(flat), -CAP, neg_m_half[:], ALU.mult, ALU.min,
             accum_out=neg_m[:],
         )
 
-        v_g = sb.tile([P, PAGES * DV], U32, name="v_g", align_bytes=64)
-        vsc_g = sb.tile([P, PAGES * DV], U8, name="vsc_g", align_bytes=64)
+        v_g = late.tile([P, PAGES * DV], U32, name="v_g", offset=0, align_bytes=64)
+        vsc_g = late.tile([P, PAGES * DV], U8, name="vsc_g", offset=PAGES * DV * 4, align_bytes=64)
         nc.vector.tensor_copy(v_g[:], v_pool[:].bitcast(U32).indirect(voffs_sb[:]))
         nc.vector.tensor_copy(vsc_g[:], vsc_pool[:].bitcast(U8).indirect(voffs_sb[:]))
 
         prob = sb.tile([P, PAGES, PACK, P], F32, name="prob")
-        l_page = sb.tile([P, PAGES], F32, name="l_page")
+        l_page = sb.tile([P, PAGES + 1], F32, name="l_page")
         w_bf = [sb.tile([P, NQ, PACK], BF16, name=f"w_bf{e}", align_bytes=64) for e in range(PAGES)]
         w_codes = [sb.tile([P, NQ], U32, name=f"w_codes{e}", align_bytes=64) for e in range(PAGES)]
         w_scales = [sb.tile([P, NQ], U8, name=f"w_scales{e}", align_bytes=64) for e in range(PAGES)]
@@ -136,11 +149,13 @@ def tile_attend_pkv8_cap_kernel(tc, qT, k_words, k_scales, v_words, v_scales, vs
             )
 
         for e in range(PAGES):
-            nc.scalar.activation(
-                prob[:, e].rearrange("q t p -> q (t p)"), neg_c[:, e].rearrange("q t p -> q (t p)"), ACT.Exp,
-                bias=neg_m[:], scale=-1.0, accum_out=l_page[:, e : e + 1],
-            )
-            turned = ps.tile([P, PACK, NQ], F32, name=f"turned{e}", tag=f"turned{e % 3}")
+            parts = ((0, 2, 0), (2, 4, PAGES)) if e == 0 else ((0, 4, e),)
+            for t0, t1, col in parts:
+                nc.scalar.activation(
+                    prob[:, e, t0:t1].rearrange("q t p -> q (t p)"), neg_c[:, e, t0:t1].rearrange("q t p -> q (t p)"),
+                    ACT.Exp, bias=neg_m[:], scale=-1.0, accum_out=l_page[:, col : col + 1],
+                )
+            turned = ps.tile([P, PACK, NQ], F32, name=f"turned{e}", tag=f"bank{e}")
             for t in range(PACK):
                 nc.tensor.transpose(turned[:, t, :], prob[:, e, t, :], ident[:])
             nc.vector.tensor_tensor(
@@ -153,7 +168,7 @@ def tile_attend_pkv8_cap_kernel(tc, qT, k_words, k_scales, v_words, v_scales, vs
                 quantize_page(e - 1)
         quantize_page(PAGES - 1)
 
-        l_copy = sb.tile([P, PAGES], F32, name="l_copy")
+        l_copy = sb.tile([P, PAGES + 1], F32, name="l_copy")
         l_sum = sb.tile([P, 1], F32, name="l_sum")
         l_inv = sb.tile([P, 1], F32, name="l_inv")
         nc.scalar.activation(l_copy[:], l_page[:], ACT.Copy, accum_out=l_sum[:])

@@ -39,44 +39,42 @@ def tile_attend_pkv8_cap_kernel(tc, qT, k_words, k_scales, v_words, v_scales, vs
         ks_pool = sb.tile([P, T // 4], I32, name="ks_pool", align_bytes=64)
         vsc_pool = sb.tile([P, POOL_PAGES * DV // 4], I32, name="vsc_pool", align_bytes=64)
         vs_pool = sb.tile([P, T], F32, name="vs_pool", align_bytes=64)
-        q_raw = sb.tile([P, PACK, NQ], F32, name="q_raw", tag="v_slot", align_bytes=64)
+        q_raw = sb.tile([P, PACK, NQ], F32, name="q_raw")
         ident = sb.tile([P, P], F32, name="ident")
-        warm = sb.tile([P, 1], F32, name="warm")
 
         nc.gpsimd.iota(diag[:], [[1, P]], base=0, channel_multiplier=-1)
         nc.vector.memset(ks_pool[:], 0)
-        nc.vector.tensor_scalar(ident[:], diag[:], 0.0, None, ALU.is_equal)
         nc.vector.memset(vs_pool[:], 0.0)
+        nc.vector.tensor_scalar(ident[:], diag[:], 0.0, None, ALU.is_equal)
         nc.vector.memset(vsc_pool[:], 0)
-        nc.scalar.activation(warm[:], ident[:, 0:1], ACT.Exp)
 
         nc.sync.dma_start(offs_sb[:], offs)
         nc.sync.dma_start(q_raw[:], qT[0].rearrange("(p j) q -> p j q", j=PACK))
         for g in range(4):
-            nc.sync.dma_start(ks_pool[32 * g : 32 * g + 4, :], k_scales[0, 4 * g : 4 * g + 4, :].bitcast(I32))
+            nc.sync.dma_start(ks_pool[g:P:32, :], k_scales[0, g:16:4, :].bitcast(I32))
+        nc.sync.dma_start(vs_pool[VS_ROW : VS_ROW + 1, :], vs[0:1, :])
         k_pool = sb.tile([P, T], I32, name="k_pool", tag="k_slot", align_bytes=64)
         nc.sync.dma_start(k_pool[:], k_words[0].rearrange("p t r -> p (t r)").bitcast(I32))
-        q_bf = sb.tile([P, NQ, PACK], BF16, name="q_bf", align_bytes=64)
+        q_bf = sb.tile([P, NQ, PACK], BF16, name="q_bf", tag="v_slot", align_bytes=64)
         q_codes = sb.tile([P, NQ], U32, name="q_codes", align_bytes=64)
         q_scales = sb.tile([P, NQ], U8, name="q_scales", align_bytes=64)
-        nc.scalar.copy(q_bf[:], q_raw[:].rearrange("p j q -> p q j"))
+        nc.scalar.activation(q_bf[:], q_raw[:].rearrange("p j q -> p q j"), ACT.Copy)
 
-        nc.scalar.dma_start(vs_pool[VS_ROW : VS_ROW + 1, :], vs[0:1, :])
         nc.sync.dma_start(voffs_sb[:], voffs)
         for g in range(4):
             nc.sync.dma_start(
-                vsc_pool[32 * g : 32 * g + 4, :].rearrange("f (u e) -> f u e", u=POOL_PAGES),
-                v_scales[:, 4 * g : 4 * g + 4, :].bitcast(I32).rearrange("u f e -> f u e"),
+                vsc_pool[g:P:32, :].rearrange("f (u e) -> f u e", u=POOL_PAGES),
+                v_scales[:, g:16:4, :].bitcast(I32).rearrange("u f e -> f u e"),
             )
+
+        ks_g = sb.tile([P, N], U8, name="ks_g", align_bytes=64)
+        nc.vector.tensor_copy(ks_g[:], ks_pool[:].bitcast(U8).indirect(offs_sb[:]))
+        nc.vector.quantize_mx(out=q_codes[:].bitcast(FP8X4), scales=q_scales[:], in_=q_bf[:].rearrange("p q j -> p (q j)"))
         v_pool = sb.tile([P, POOL_PAGES * DV], I32, name="v_pool", tag="v_slot", align_bytes=64)
         nc.sync.dma_start(
             v_pool[:].rearrange("p (u e) -> p u e", u=POOL_PAGES),
             v_words.rearrange("u p e r -> p u (e r)").bitcast(I32),
         )
-
-        ks_g = sb.tile([P, N], U8, name="ks_g", align_bytes=64)
-        nc.vector.tensor_copy(ks_g[:], ks_pool[:].bitcast(U8).indirect(offs_sb[:]))
-        nc.vector.quantize_mx(out=q_codes[:].bitcast(FP8X4), scales=q_scales[:], in_=q_bf[:].rearrange("p q j -> p (q j)"))
 
         vs_t = [sb.tile([P, 1, PACK], F32, name=f"vs_t{e}") for e in range(PAGES)]
 
@@ -92,6 +90,7 @@ def tile_attend_pkv8_cap_kernel(tc, qT, k_words, k_scales, v_words, v_scales, vs
 
         gather_token_scales(0, "vs_g0")
         gather_token_scales(1, "vs_g1")
+        gather_token_scales(2, "vs_g2")
 
         k_g = [sb.tile([P, PAGE], U32, name=f"k_g{e}", tag=f"k_g{e}", align_bytes=64) for e in range(PAGES)]
         th_lo = sb.tile([P, 2, PACK, P], F32, name="th_lo")
@@ -116,8 +115,7 @@ def tile_attend_pkv8_cap_kernel(tc, qT, k_words, k_scales, v_words, v_scales, vs
                 th[e], score[:].rearrange("q (p t) -> q t p", t=PACK), ACT.Tanh, scale=1.0 / CAP
             )
 
-        gather_token_scales(2, "k_g0")
-        gather_token_scales(3, "k_g1")
+        gather_token_scales(3, "k_g0")
 
         neg_c = sb.tile([P, PAGES, PACK, P], F32, name="neg_c")
         neg_m_half = sb.tile([P, 1], F32, name="neg_m_half")

@@ -23,84 +23,78 @@ P = 128
 PACK = 4
 PAGES = N // PAGE
 POOL_PAGES = T // PAGE
-VS_ROW = 8
 
 
 def tile_attend_pkv8_cap_kernel(tc, qT, k_words, k_scales, v_words, v_scales, vs, offs, voffs, out):
     nc = tc.nc
     with ExitStack() as ctx:
         sb = ctx.enter_context(tc.tile_pool(name="sb", bufs=1))
-        late = ctx.enter_context(tc.tile_pool(name="late", bufs=1))
+        shared = ctx.enter_context(tc.tile_pool(name="shared", bufs=1))
         ps = ctx.enter_context(tc.psum_pool(name="ps", bufs=1))
+
+        vs_bytes = T * 4
+        v_bytes = POOL_PAGES * DV * 4
+        q_bf_bytes = NQ * PACK * 2
 
         offs_sb = sb.tile([P, N // 16], U16, name="offs_sb")
         voffs_sb = sb.tile([P, PAGES * DV // 16], U16, name="voffs_sb")
         diag = sb.tile([P, P], I32, name="diag", tag="k_slot", align_bytes=64)
         ks_pool = sb.tile([P, T // 4], I32, name="ks_pool", align_bytes=64)
-        vsc_pool = sb.tile([P, POOL_PAGES * DV // 4], I32, name="vsc_pool", align_bytes=64)
-        vs_pool = sb.tile([P, T], F32, name="vs_pool", align_bytes=64)
-        q_raw = sb.tile([P, PACK, NQ], F32, name="q_raw")
+        q_raw = shared.tile([P, PACK, NQ], F32, name="q_raw", offset=0, align_bytes=64)
         ident = sb.tile([P, P], F32, name="ident")
 
         nc.gpsimd.iota(diag[:], [[1, P]], base=0, channel_multiplier=-1)
         nc.vector.memset(ks_pool[:], 0)
-        nc.vector.memset(vs_pool[:], 0.0)
         nc.vector.tensor_scalar(ident[:], diag[:], 0.0, None, ALU.is_equal)
-        nc.vector.memset(vsc_pool[:], 0)
 
         nc.sync.dma_start(offs_sb[:], offs)
         nc.sync.dma_start(q_raw[:], qT[0].rearrange("(p j) q -> p j q", j=PACK))
         for g in range(4):
             nc.sync.dma_start(ks_pool[g:P:32, :], k_scales[0, g:16:4, :].bitcast(I32))
-        nc.sync.dma_start(vs_pool[VS_ROW : VS_ROW + 1, :], vs[0:1, :])
         k_pool = sb.tile([P, T], I32, name="k_pool", tag="k_slot", align_bytes=64)
         nc.sync.dma_start(k_pool[:], k_words[0].rearrange("p t r -> p (t r)").bitcast(I32))
-        q_bf = sb.tile([P, NQ, PACK], BF16, name="q_bf", tag="v_slot", align_bytes=64)
+        nc.sync.dma_start(voffs_sb[:], voffs)
+
+        q_bf = shared.tile(
+            [P, NQ, PACK], BF16, name="q_bf", offset=vs_bytes + v_bytes - q_bf_bytes // 2, align_bytes=64
+        )
         q_codes = sb.tile([P, NQ], U32, name="q_codes", align_bytes=64)
         q_scales = sb.tile([P, NQ], U8, name="q_scales", align_bytes=64)
         nc.scalar.activation(q_bf[:], q_raw[:].rearrange("p j q -> p q j"), ACT.Copy)
 
-        nc.sync.dma_start(voffs_sb[:], voffs)
+        vs_pool = shared.tile([P, T], F32, name="vs_pool", offset=0, align_bytes=64)
+        nc.sync.dma_start(vs_pool[:], vs)
+
+        ks_g = sb.tile([P, N], U8, name="ks_g", align_bytes=64)
+        nc.vector.tensor_copy(ks_g[:], ks_pool[:].bitcast(U8).indirect(offs_sb[:]))
+        nc.vector.quantize_mx(out=q_codes[:].bitcast(FP8X4), scales=q_scales[:], in_=q_bf[:].rearrange("p q j -> p (q j)"))
+
+        v_pool = shared.tile([P, POOL_PAGES * DV], I32, name="v_pool", offset=vs_bytes, align_bytes=64)
+        vsc_pool = shared.tile(
+            [P, POOL_PAGES * DV // 4], I32, name="vsc_pool", offset=vs_bytes + v_bytes, align_bytes=64
+        )
+        nc.sync.dma_start(
+            v_pool[:].rearrange("p (u e) -> p u e", u=POOL_PAGES),
+            v_words.rearrange("u p e r -> p u (e r)").bitcast(I32),
+        )
+        nc.vector.memset(vsc_pool[:], 0)
         for g in range(4):
             nc.sync.dma_start(
                 vsc_pool[g:P:32, :].rearrange("f (u e) -> f u e", u=POOL_PAGES),
                 v_scales[:, g:16:4, :].bitcast(I32).rearrange("u f e -> f u e"),
             )
 
-        ks_g = sb.tile([P, N], U8, name="ks_g", align_bytes=64)
-        nc.vector.tensor_copy(ks_g[:], ks_pool[:].bitcast(U8).indirect(offs_sb[:]))
-        nc.vector.quantize_mx(out=q_codes[:].bitcast(FP8X4), scales=q_scales[:], in_=q_bf[:].rearrange("p q j -> p (q j)"))
-        v_pool = sb.tile([P, POOL_PAGES * DV], I32, name="v_pool", tag="v_slot", align_bytes=64)
-        nc.sync.dma_start(
-            v_pool[:].rearrange("p (u e) -> p u e", u=POOL_PAGES),
-            v_words.rearrange("u p e r -> p u (e r)").bitcast(I32),
-        )
-
-        vs_t = [sb.tile([P, 1, PACK], F32, name=f"vs_t{e}") for e in range(PAGES)]
-
         def page_offsets(e):
             return offs_sb[:, e * PAGE // 16 : (e + 1) * PAGE // 16]
 
-        def gather_token_scales(e, tag):
-            vs_g = sb.tile([P, PAGE], F32, name=f"vs_g{e}", tag=tag, align_bytes=64)
-            nc.vector.tensor_copy(vs_g[:], vs_pool[:].indirect(page_offsets(e)))
-            nc.sync.dma_start(
-                vs_t[e][:, 0, :], vs_g[VS_ROW : VS_ROW + 1, :].rearrange("o (p t) -> o p t", t=PACK)
-            )
-
-        gather_token_scales(0, "vs_g0")
-        gather_token_scales(1, "vs_g1")
-        gather_token_scales(2, "vs_g2")
-
-        k_g = [sb.tile([P, PAGE], U32, name=f"k_g{e}", tag=f"k_g{e}", align_bytes=64) for e in range(PAGES)]
-        th_lo = sb.tile([P, 2, PACK, P], F32, name="th_lo")
-        th_hi = late.tile([P, 2, PACK, P], F32, name="th_hi", offset=0, align_bytes=64)
-        th = [th_lo[:, 0], th_lo[:, 1], th_hi[:, 0], th_hi[:, 1]]
+        k_g = [sb.tile([P, PAGE], U32, name=f"k_g{e}", align_bytes=64) for e in range(PAGES)]
+        th = [sb.tile([P, PAGE + 1], F32, name=f"th{e}", align_bytes=64) for e in range(PAGES)]
+        ex = [sb.tile([P, PAGE], F32, name=f"ex{e}", align_bytes=64) for e in range(PAGES)]
+        th_max = sb.tile([P, 1], F32, name="th_max")
+        l_page = sb.tile([P, PAGES], F32, name="l_page")
         for e in range(PAGES):
             cols = slice(e * PAGE, (e + 1) * PAGE)
-            nc.vector.tensor_copy(
-                k_g[e][:], k_pool[:].bitcast(U32).indirect(page_offsets(e))
-            )
+            nc.vector.tensor_copy(k_g[e][:], k_pool[:].bitcast(U32).indirect(page_offsets(e)))
             score = ps.tile([P, PAGE], F32, name=f"score{e}", tag=f"bank{e}")
             nc.tensor.matmul_mx(
                 out=score[:],
@@ -111,65 +105,51 @@ def tile_attend_pkv8_cap_kernel(tc, qT, k_words, k_scales, v_words, v_scales, vs
                 start=True,
                 stop=True,
             )
-            nc.scalar.activation(
-                th[e], score[:].rearrange("q (p t) -> q t p", t=PACK), ACT.Tanh, scale=1.0 / CAP
-            )
+            nc.scalar.activation(th[e][:, :PAGE], score[:], ACT.Tanh, scale=1.0 / CAP)
+            nc.scalar.activation(ex[e][:], th[e][:, :PAGE], ACT.Exp, scale=CAP, accum_out=l_page[:, e : e + 1])
 
-        gather_token_scales(3, "k_g0")
+        for e in range(PAGES):
+            width = PAGE if e == 0 else PAGE + 1
+            so_far = th[e + 1][:, PAGE : PAGE + 1] if e + 1 < PAGES else th_max[:]
+            nc.vector.tensor_reduce(so_far, th[e][:, :width], mybir.AxisListType.X, ALU.max)
 
-        neg_c = sb.tile([P, PAGES, PACK, P], F32, name="neg_c")
-        neg_m_half = sb.tile([P, 1], F32, name="neg_m_half")
-        neg_m = sb.tile([P, 1], F32, name="neg_m")
-        flat = "q e t p -> q (e t p)"
-        nc.vector.tensor_scalar(
-            neg_c[:, 0:2].rearrange(flat), th_lo[:].rearrange(flat), -CAP, None, ALU.mult, ALU.min,
-            accum_out=neg_m_half[:],
-        )
-        nc.vector.tensor_scalar(
-            neg_c[:, 2:4].rearrange(flat), th_hi[:].rearrange(flat), -CAP, neg_m_half[:], ALU.mult, ALU.min,
-            accum_out=neg_m[:],
-        )
+        exp_neg_m = sb.tile([P, 1], F32, name="exp_neg_m")
+        nc.scalar.activation(exp_neg_m[:], th_max[:], ACT.Exp, scale=-CAP)
 
-        v_g = late.tile([P, PAGES * DV], U32, name="v_g", offset=0, align_bytes=64)
-        vsc_g = late.tile([P, PAGES * DV], U8, name="vsc_g", offset=PAGES * DV * 4, align_bytes=64)
-        nc.vector.tensor_copy(v_g[:], v_pool[:].bitcast(U32).indirect(voffs_sb[:]))
-        nc.vector.tensor_copy(vsc_g[:], vsc_pool[:].bitcast(U8).indirect(voffs_sb[:]))
-
-        prob = sb.tile([P, PAGES, PACK, P], F32, name="prob")
-        l_page = sb.tile([P, PAGES + 1], F32, name="l_page")
+        w_f32 = [sb.tile([P, PAGE], F32, name=f"w_f32{e}", align_bytes=64) for e in range(PAGES)]
+        w_row = [sb.tile([P, 2, P, 2], BF16, name=f"w_row{e}", align_bytes=64) for e in range(PAGES)]
         w_bf = [sb.tile([P, NQ, PACK], BF16, name=f"w_bf{e}", align_bytes=64) for e in range(PAGES)]
         w_codes = [sb.tile([P, NQ], U32, name=f"w_codes{e}", align_bytes=64) for e in range(PAGES)]
         w_scales = [sb.tile([P, NQ], U8, name=f"w_scales{e}", align_bytes=64) for e in range(PAGES)]
+        for e in range(PAGES):
+            nc.vector.tensor_tensor(w_f32[e][:], vs_pool[:].indirect(page_offsets(e)), ex[e][:], ALU.mult)
 
-        def quantize_page(e):
+        v_g = sb.tile([P, PAGES * DV], U32, name="v_g", align_bytes=64)
+        vsc_g = sb.tile([P, PAGES * DV], U8, name="vsc_g", align_bytes=64)
+        nc.vector.tensor_copy(v_g[:], v_pool[:].bitcast(U32).indirect(voffs_sb[:]))
+        nc.vector.tensor_copy(vsc_g[:], vsc_pool[:].bitcast(U8).indirect(voffs_sb[:]))
+
+        for e in range(PAGES):
+            nc.scalar.activation(
+                w_row[e][:], w_f32[e][:].rearrange("q (p u j) -> q u p j", u=2, j=2), ACT.Copy, scale=exp_neg_m[:]
+            )
+            turned = ps.tile([P, 2, NQ], F32, name=f"turned{e}", tag=f"bank{e}")
+            for u in range(2):
+                nc.tensor.transpose(
+                    turned[:, u, :], w_row[e][:, u].rearrange("q p j -> q (p j)").bitcast(F32), ident[:]
+                )
+            nc.scalar.copy(
+                w_bf[e][:].rearrange("p q t -> p (q t)").bitcast(F32).rearrange("p (q u) -> p q u", u=2),
+                turned[:].rearrange("p u q -> p q u"),
+            )
             nc.vector.quantize_mx(
                 out=w_codes[e][:].bitcast(FP8X4), scales=w_scales[e][:], in_=w_bf[e][:].rearrange("p q t -> p (q t)")
             )
 
-        for e in range(PAGES):
-            parts = ((0, 2, 0), (2, 4, PAGES)) if e == 0 else ((0, 4, e),)
-            for t0, t1, col in parts:
-                nc.scalar.activation(
-                    prob[:, e, t0:t1].rearrange("q t p -> q (t p)"), neg_c[:, e, t0:t1].rearrange("q t p -> q (t p)"),
-                    ACT.Exp, bias=neg_m[:], scale=-1.0, accum_out=l_page[:, col : col + 1],
-                )
-            turned = ps.tile([P, PACK, NQ], F32, name=f"turned{e}", tag=f"bank{e}")
-            for t in range(PACK):
-                nc.tensor.transpose(turned[:, t, :], prob[:, e, t, :], ident[:])
-            nc.vector.tensor_tensor(
-                w_bf[e][:],
-                turned[:].rearrange("p t q -> p q t"),
-                vs_t[e][:].to_broadcast([P, NQ, PACK]),
-                ALU.mult,
-            )
-            if e > 0:
-                quantize_page(e - 1)
-        quantize_page(PAGES - 1)
-
-        l_copy = sb.tile([P, PAGES + 1], F32, name="l_copy")
+        l_scaled = sb.tile([P, PAGES], F32, name="l_scaled")
         l_sum = sb.tile([P, 1], F32, name="l_sum")
         l_inv = sb.tile([P, 1], F32, name="l_inv")
-        nc.scalar.activation(l_copy[:], l_page[:], ACT.Copy, accum_out=l_sum[:])
+        nc.scalar.activation(l_scaled[:], l_page[:], ACT.Copy, scale=exp_neg_m[:], accum_out=l_sum[:])
         nc.vector.reciprocal(l_inv[:], l_sum[:])
 
         acc = ps.tile([P, DV], F32, name="acc")

@@ -29,55 +29,46 @@ def tile_attend_pkv8_cap_kernel(tc, qT, k_words, k_scales, v_words, v_scales, vs
     nc = tc.nc
     with ExitStack() as ctx:
         sb = ctx.enter_context(tc.tile_pool(name="sb", bufs=1))
-        shared = ctx.enter_context(tc.tile_pool(name="shared", bufs=1))
         ps = ctx.enter_context(tc.psum_pool(name="ps", bufs=1))
-
-        vs_bytes = T * 4
-        v_bytes = POOL_PAGES * DV * 4
-        q_bf_bytes = NQ * PACK * 2
 
         offs_sb = sb.tile([P, N // 16], U16, name="offs_sb")
         voffs_sb = sb.tile([P, PAGES * DV // 16], U16, name="voffs_sb")
-        diag = sb.tile([P, P], I32, name="diag", tag="k_slot", align_bytes=64)
+        diag = sb.tile([P, P], I32, name="diag")
         ks_pool = sb.tile([P, T // 4], I32, name="ks_pool", align_bytes=64)
-        q_raw = shared.tile([P, PACK, NQ], F32, name="q_raw", offset=0, align_bytes=64)
+        q_raw = sb.tile([P, PACK, NQ], F32, name="q_raw")
+        vsc_pool = sb.tile([P, POOL_PAGES * DV // 4], I32, name="vsc_pool", align_bytes=64)
         ident = sb.tile([P, P], F32, name="ident")
 
         nc.gpsimd.iota(diag[:], [[1, P]], base=0, channel_multiplier=-1)
         nc.vector.memset(ks_pool[:], 0)
+        nc.vector.memset(vsc_pool[:], 0)
         nc.vector.tensor_scalar(ident[:], diag[:], 0.0, None, ALU.is_equal)
 
         nc.sync.dma_start(offs_sb[:], offs)
         nc.sync.dma_start(q_raw[:], qT[0].rearrange("(p j) q -> p j q", j=PACK))
+        nc.sync.dma_start(voffs_sb[:], voffs)
         for g in range(4):
             nc.sync.dma_start(ks_pool[g:P:32, :], k_scales[0, g:16:4, :].bitcast(I32))
-        k_pool = sb.tile([P, T], I32, name="k_pool", tag="k_slot", align_bytes=64)
+        k_pool = sb.tile([P, T], I32, name="k_pool", align_bytes=64)
         nc.sync.dma_start(k_pool[:], k_words[0].rearrange("p t r -> p (t r)").bitcast(I32))
-        nc.sync.dma_start(voffs_sb[:], voffs)
 
-        q_bf = shared.tile(
-            [P, NQ, PACK], BF16, name="q_bf", offset=vs_bytes + v_bytes - q_bf_bytes // 2, align_bytes=64
-        )
+        q_bf = sb.tile([P, NQ, PACK], BF16, name="q_bf", align_bytes=64)
         q_codes = sb.tile([P, NQ], U32, name="q_codes", align_bytes=64)
         q_scales = sb.tile([P, NQ], U8, name="q_scales", align_bytes=64)
         nc.scalar.activation(q_bf[:], q_raw[:].rearrange("p j q -> p q j"), ACT.Copy)
 
-        vs_pool = shared.tile([P, T], F32, name="vs_pool", offset=0, align_bytes=64)
+        vs_pool = sb.tile([P, T], F32, name="vs_pool", align_bytes=64)
         nc.sync.dma_start(vs_pool[:], vs)
 
         ks_g = sb.tile([P, N], U8, name="ks_g", align_bytes=64)
         nc.vector.tensor_copy(ks_g[:], ks_pool[:].bitcast(U8).indirect(offs_sb[:]))
         nc.vector.quantize_mx(out=q_codes[:].bitcast(FP8X4), scales=q_scales[:], in_=q_bf[:].rearrange("p q j -> p (q j)"))
 
-        v_pool = shared.tile([P, POOL_PAGES * DV], I32, name="v_pool", offset=vs_bytes, align_bytes=64)
-        vsc_pool = shared.tile(
-            [P, POOL_PAGES * DV // 4], I32, name="vsc_pool", offset=vs_bytes + v_bytes, align_bytes=64
-        )
+        v_pool = sb.tile([P, POOL_PAGES * DV], I32, name="v_pool", align_bytes=64)
         nc.sync.dma_start(
             v_pool[:].rearrange("p (u e) -> p u e", u=POOL_PAGES),
             v_words.rearrange("u p e r -> p u (e r)").bitcast(I32),
         )
-        nc.vector.memset(vsc_pool[:], 0)
         for g in range(4):
             nc.sync.dma_start(
                 vsc_pool[g:P:32, :].rearrange("f (u e) -> f u e", u=POOL_PAGES),

@@ -57,6 +57,11 @@ def tile_attend_pkv8_cap_kernel(tc, qT, k_words, k_scales, v_words, v_scales, vs
         q_scales = sb.tile([P, NQ], U8, name="q_scales", align_bytes=64)
         nc.scalar.activation(q_bf[:], q_raw[:].rearrange("p j q -> p q j"), ACT.Copy)
 
+        for g in range(4):
+            nc.sync.dma_start(
+                vsc_pool[g:P:32, :].rearrange("f (u e) -> f u e", u=POOL_PAGES),
+                v_scales[:, g:16:4, :].bitcast(I32).rearrange("u f e -> f u e"),
+            )
         vs_pool = sb.tile([P, T], F32, name="vs_pool", align_bytes=64)
         nc.sync.dma_start(vs_pool[:], vs)
 
@@ -69,20 +74,21 @@ def tile_attend_pkv8_cap_kernel(tc, qT, k_words, k_scales, v_words, v_scales, vs
             v_pool[:].rearrange("p (u e) -> p u e", u=POOL_PAGES),
             v_words.rearrange("u p e r -> p u (e r)").bitcast(I32),
         )
-        for g in range(4):
-            nc.sync.dma_start(
-                vsc_pool[g:P:32, :].rearrange("f (u e) -> f u e", u=POOL_PAGES),
-                v_scales[:, g:16:4, :].bitcast(I32).rearrange("u f e -> f u e"),
-            )
 
         def page_offsets(e):
             return offs_sb[:, e * PAGE // 16 : (e + 1) * PAGE // 16]
 
         k_g = [sb.tile([P, PAGE], U32, name=f"k_g{e}", align_bytes=64) for e in range(PAGES)]
-        th = [sb.tile([P, PAGE + 1], F32, name=f"th{e}", align_bytes=64) for e in range(PAGES)]
-        ex = [sb.tile([P, PAGE], F32, name=f"ex{e}", align_bytes=64) for e in range(PAGES)]
-        th_max = sb.tile([P, 1], F32, name="th_max")
+        last = PAGES - 1
+        th = [
+            sb.tile([P, PAGE + (last if e == last else 0)], F32, name=f"th{e}", tag=f"th{e}", align_bytes=64) for e in range(PAGES)
+        ]
+        ex = [sb.tile([P, PAGE], F32, name=f"ex{e}", tag=f"ex{e}", align_bytes=64) for e in range(PAGES)]
         l_page = sb.tile([P, PAGES], F32, name="l_page")
+
+        def exp_page(e):
+            nc.scalar.activation(ex[e][:], th[e][:, :PAGE], ACT.Exp, scale=CAP, accum_out=l_page[:, e : e + 1])
+
         for e in range(PAGES):
             cols = slice(e * PAGE, (e + 1) * PAGE)
             nc.vector.tensor_copy(k_g[e][:], k_pool[:].bitcast(U32).indirect(page_offsets(e)))
@@ -97,32 +103,38 @@ def tile_attend_pkv8_cap_kernel(tc, qT, k_words, k_scales, v_words, v_scales, vs
                 stop=True,
             )
             nc.scalar.activation(th[e][:, :PAGE], score[:], ACT.Tanh, scale=1.0 / CAP)
-            nc.scalar.activation(ex[e][:], th[e][:, :PAGE], ACT.Exp, scale=CAP, accum_out=l_page[:, e : e + 1])
+            if e < PAGES - 2:
+                exp_page(e)
+        exp_page(PAGES - 2)
+        exp_page(PAGES - 1)
 
-        for e in range(PAGES):
-            width = PAGE if e == 0 else PAGE + 1
-            so_far = th[e + 1][:, PAGE : PAGE + 1] if e + 1 < PAGES else th_max[:]
-            nc.vector.tensor_reduce(so_far, th[e][:, :width], mybir.AxisListType.X, ALU.max)
+        for e in range(last):
+            nc.vector.tensor_reduce(th[last][:, PAGE + e : PAGE + e + 1], th[e][:], mybir.AxisListType.X, ALU.max)
 
-        exp_neg_m = sb.tile([P, 1], F32, name="exp_neg_m")
-        nc.scalar.activation(exp_neg_m[:], th_max[:], ACT.Exp, scale=-CAP)
-
-        w_f32 = [sb.tile([P, PAGE], F32, name=f"w_f32{e}", align_bytes=64) for e in range(PAGES)]
+        w_f32 = [sb.tile([P, PAGE], F32, name=f"w_f32{e}", align_bytes=64)[:] for e in range(PAGES)]
         w_row = [sb.tile([P, 2, P, 2], BF16, name=f"w_row{e}", align_bytes=64) for e in range(PAGES)]
         w_bf = [sb.tile([P, NQ, PACK], BF16, name=f"w_bf{e}", align_bytes=64) for e in range(PAGES)]
         w_codes = [sb.tile([P, NQ], U32, name=f"w_codes{e}", align_bytes=64) for e in range(PAGES)]
         w_scales = [sb.tile([P, NQ], U8, name=f"w_scales{e}", align_bytes=64) for e in range(PAGES)]
-        for e in range(PAGES):
-            nc.vector.tensor_tensor(w_f32[e][:], vs_pool[:].indirect(page_offsets(e)), ex[e][:], ALU.mult)
 
-        v_g = sb.tile([P, PAGES * DV], U32, name="v_g", align_bytes=64)
-        vsc_g = sb.tile([P, PAGES * DV], U8, name="vsc_g", align_bytes=64)
+        def weigh_page(e):
+            nc.vector.tensor_tensor(w_f32[e], vs_pool[:].indirect(page_offsets(e)), ex[e][:], ALU.mult)
+
+        th_max = sb.tile([P, 1], F32, name="th_max")
+        nc.vector.tensor_reduce(th_max[:], th[last][:], mybir.AxisListType.X, ALU.max)
+        exp_neg_m = sb.tile([P, 1], F32, name="exp_neg_m")
+        nc.scalar.activation(exp_neg_m[:], th_max[:], ACT.Exp, scale=-CAP)
+        for e in range(PAGES):
+            weigh_page(e)
+
+        v_g = sb.tile([P, PAGES * DV], U32, name="v_g", tag=f"ex{last - 1}", align_bytes=64)
+        vsc_g = sb.tile([P, PAGES * DV], U8, name="vsc_g", tag=f"ex{last}", align_bytes=64)
         nc.vector.tensor_copy(v_g[:], v_pool[:].bitcast(U32).indirect(voffs_sb[:]))
         nc.vector.tensor_copy(vsc_g[:], vsc_pool[:].bitcast(U8).indirect(voffs_sb[:]))
 
         for e in range(PAGES):
             nc.scalar.activation(
-                w_row[e][:], w_f32[e][:].rearrange("q (p u j) -> q u p j", u=2, j=2), ACT.Copy, scale=exp_neg_m[:]
+                w_row[e][:], w_f32[e].rearrange("q (p u j) -> q u p j", u=2, j=2), ACT.Copy, scale=exp_neg_m[:]
             )
             turned = ps.tile([P, 2, NQ], F32, name=f"turned{e}", tag=f"bank{e}")
             for u in range(2):
@@ -139,11 +151,11 @@ def tile_attend_pkv8_cap_kernel(tc, qT, k_words, k_scales, v_words, v_scales, vs
 
         l_scaled = sb.tile([P, PAGES], F32, name="l_scaled")
         l_sum = sb.tile([P, 1], F32, name="l_sum")
-        l_inv = sb.tile([P, 1], F32, name="l_inv")
+        l_inv = sb.tile([P, 1], F32, name="l_inv", tag="ex0", align_bytes=64)
         nc.scalar.activation(l_scaled[:], l_page[:], ACT.Copy, scale=exp_neg_m[:], accum_out=l_sum[:])
         nc.vector.reciprocal(l_inv[:], l_sum[:])
 
-        acc = ps.tile([P, DV], F32, name="acc")
+        acc = ps.tile([P, DV], F32, name="acc", tag=f"bank{last}")
         for e in range(PAGES):
             cols = slice(e * DV, (e + 1) * DV)
             nc.tensor.matmul_mx(

@@ -37,6 +37,7 @@ def tile_attend_pkv8_cap_kernel(tc, qT, k_words, k_scales, v_words, v_scales, vs
         ks_pool = sb.tile([P, T // 4], I32, name="ks_pool", align_bytes=64)
         q_raw = sb.tile([P, PACK, NQ], F32, name="q_raw")
         vsc_pool = sb.tile([P, POOL_PAGES * DV // 4], I32, name="vsc_pool", align_bytes=64)
+        vs_cols = sb.tile([P, T // P], F32, name="vs_cols")
         ident = sb.tile([P, P], F32, name="ident")
 
         nc.gpsimd.iota(diag[:], [[1, P]], base=0, channel_multiplier=-1)
@@ -46,11 +47,12 @@ def tile_attend_pkv8_cap_kernel(tc, qT, k_words, k_scales, v_words, v_scales, vs
 
         nc.sync.dma_start(offs_sb[:], offs)
         nc.sync.dma_start(q_raw[:], qT[0].rearrange("(p j) q -> p j q", j=PACK))
-        nc.sync.dma_start(voffs_sb[:], voffs)
+        nc.sync.dma_start(vs_cols[:], vs[0].rearrange("(p j) -> p j", p=P))
         for g in range(4):
             nc.sync.dma_start(ks_pool[g:P:32, :], k_scales[0, g:16:4, :].bitcast(I32))
         k_pool = sb.tile([P, T], I32, name="k_pool", align_bytes=64)
         nc.sync.dma_start(k_pool[:], k_words[0].rearrange("p t r -> p (t r)").bitcast(I32))
+        nc.sync.dma_start(voffs_sb[:], voffs)
 
         q_bf = sb.tile([P, NQ, PACK], BF16, name="q_bf", align_bytes=64)
         q_codes = sb.tile([P, NQ], U32, name="q_codes", align_bytes=64)
@@ -63,7 +65,13 @@ def tile_attend_pkv8_cap_kernel(tc, qT, k_words, k_scales, v_words, v_scales, vs
                 v_scales[:, g:16:4, :].bitcast(I32).rearrange("u f e -> f u e"),
             )
         vs_pool = sb.tile([P, T], F32, name="vs_pool", align_bytes=64)
-        nc.sync.dma_start(vs_pool[:], vs)
+        vs_runs = vs_pool[:].rearrange("q (p b t) -> q b p t", p=P, t=PACK)
+        for b in range(T // P // PACK):
+            spread = ps.tile([P, PACK, P], F32, name=f"spread{b}", tag=f"spread{b % 4}")
+            for t in range(PACK):
+                j = PACK * b + t
+                nc.tensor.transpose(spread[:, t, :], vs_cols[:, j : j + 1].to_broadcast([P, P]), ident[:])
+            nc.scalar.activation(vs_runs[:, b], spread[:].rearrange("q t p -> q p t"), ACT.Copy)
 
         ks_g = sb.tile([P, N], U8, name="ks_g", align_bytes=64)
         nc.vector.tensor_copy(ks_g[:], ks_pool[:].bitcast(U8).indirect(offs_sb[:]))

@@ -1,6 +1,7 @@
 from contextlib import ExitStack
 
 import concourse.mybir as mybir
+from concourse.masks import make_identity
 
 N, T, D, DV, NQ = 2048, 4096, 512, 128, 128
 PAGE = 512
@@ -31,39 +32,58 @@ def tile_attend_pkv8_cap_kernel(tc, qT, k_words, k_scales, v_words, v_scales, vs
         sb = ctx.enter_context(tc.tile_pool(name="sb", bufs=1))
         ps = ctx.enter_context(tc.psum_pool(name="ps", bufs=1))
 
+        half = N // 2
         offs_sb = sb.tile([P, N // 16], U16, name="offs_sb")
         voffs_sb = sb.tile([P, PAGES * DV // 16], U16, name="voffs_sb")
-        diag = sb.tile([P, P], I32, name="diag")
         ks_pool = sb.tile([P, T // 4], I32, name="ks_pool", align_bytes=64)
-        q_raw = sb.tile([P, PACK, NQ], F32, name="q_raw")
         vsc_pool = sb.tile([P, POOL_PAGES * DV // 4], I32, name="vsc_pool", align_bytes=64)
+        ks_plane = [sb.tile([P, half // 4], I32, name=f"ks_plane{h}", align_bytes=64) for h in range(2)]
+        vsc_plane = sb.tile([P, PAGES * DV // 4], I32, name="vsc_plane", align_bytes=64)
+        q_raw = sb.tile([P, PACK, NQ], F32, name="q_raw")
         vs_cols = sb.tile([P, T // P], F32, name="vs_cols")
+        k_pool = sb.tile([P, T], I32, name="k_pool", align_bytes=64)
+        v_pool = sb.tile([P, POOL_PAGES * DV], I32, name="v_pool", align_bytes=64)
         ident = sb.tile([P, P], F32, name="ident")
 
-        nc.gpsimd.iota(diag[:], [[1, P]], base=0, channel_multiplier=-1)
-        nc.vector.memset(ks_pool[:], 0)
-        nc.vector.memset(vsc_pool[:], 0)
-        nc.vector.tensor_scalar(ident[:], diag[:], 0.0, None, ALU.is_equal)
+        make_identity(nc, ident[:])
+        for zeroed in (vsc_pool, ks_pool, ks_plane[0], ks_plane[1], vsc_plane):
+            nc.vector.memset(zeroed[:], 0)
 
         nc.sync.dma_start(offs_sb[:], offs)
-        nc.sync.dma_start(q_raw[:], qT[0].rearrange("(p j) q -> p j q", j=PACK))
-        nc.sync.dma_start(vs_cols[:], vs[0].rearrange("(p j) -> p j", p=P))
-        for g in range(4):
-            nc.sync.dma_start(ks_pool[g:P:32, :], k_scales[0, g:16:4, :].bitcast(I32))
-        k_pool = sb.tile([P, T], I32, name="k_pool", align_bytes=64)
-        nc.sync.dma_start(k_pool[:], k_words[0].rearrange("p t r -> p (t r)").bitcast(I32))
         nc.sync.dma_start(voffs_sb[:], voffs)
+        nc.sync.dma_start(
+            vsc_pool[0:P:8, :].rearrange("f (u e) -> f u e", u=POOL_PAGES),
+            v_scales.bitcast(I32).rearrange("u f e -> f u e"),
+        )
+        nc.sync.dma_start(q_raw[:], qT[0].rearrange("(p j) q -> p j q", j=PACK))
+        nc.sync.dma_start(ks_pool[0:P:8, :], k_scales[0].bitcast(I32))
+        nc.sync.dma_start(vs_cols[:], vs[0].rearrange("(p j) -> p j", p=P))
+        nc.sync.dma_start(k_pool[:], k_words[0].rearrange("p t r -> p (t r)").bitcast(I32))
 
         q_bf = sb.tile([P, NQ, PACK], BF16, name="q_bf", align_bytes=64)
         q_codes = sb.tile([P, NQ], U32, name="q_codes", align_bytes=64)
         q_scales = sb.tile([P, NQ], U8, name="q_scales", align_bytes=64)
         nc.scalar.activation(q_bf[:], q_raw[:].rearrange("p j q -> p q j"), ACT.Copy)
 
-        for g in range(4):
-            nc.sync.dma_start(
-                vsc_pool[g:P:32, :].rearrange("f (u e) -> f u e", u=POOL_PAGES),
-                v_scales[:, g:16:4, :].bitcast(I32).rearrange("u f e -> f u e"),
+        def place_scale_rows(plane, gathered):
+            for g in range(4):
+                nc.sync.dma_start(plane[g:P:32, :], gathered[8 * g : P : 32, :].bitcast(I32))
+
+        vsc_g = sb.tile([P, PAGES * DV], U8, name="vsc_g", align_bytes=64)
+        nc.vector.tensor_copy(vsc_g[:], vsc_pool[:].bitcast(U8).indirect(voffs_sb[:]))
+        for h in range(2):
+            ks_g = sb.tile([P, half], U8, name=f"ks_g{h}", align_bytes=64)
+            nc.vector.tensor_copy(
+                ks_g[:], ks_pool[:].bitcast(U8).indirect(offs_sb[:, h * half // 16 : (h + 1) * half // 16])
             )
+            place_scale_rows(ks_plane[h], ks_g)
+        nc.vector.quantize_mx(out=q_codes[:].bitcast(FP8X4), scales=q_scales[:], in_=q_bf[:].rearrange("p q j -> p (q j)"))
+        nc.sync.dma_start(
+            v_pool[:].rearrange("p (u e) -> p u e", u=POOL_PAGES),
+            v_words.rearrange("u p e r -> p u (e r)").bitcast(I32),
+        )
+        place_scale_rows(vsc_plane, vsc_g)
+
         vs_pool = sb.tile([P, T], F32, name="vs_pool", align_bytes=64)
         vs_runs = vs_pool[:].rearrange("q (p b t) -> q b p t", p=P, t=PACK)
         for b in range(T // P // PACK):
@@ -72,16 +92,6 @@ def tile_attend_pkv8_cap_kernel(tc, qT, k_words, k_scales, v_words, v_scales, vs
                 j = PACK * b + t
                 nc.tensor.transpose(spread[:, t, :], vs_cols[:, j : j + 1].to_broadcast([P, P]), ident[:])
             nc.scalar.activation(vs_runs[:, b], spread[:].rearrange("q t p -> q p t"), ACT.Copy)
-
-        ks_g = sb.tile([P, N], U8, name="ks_g", align_bytes=64)
-        nc.vector.tensor_copy(ks_g[:], ks_pool[:].bitcast(U8).indirect(offs_sb[:]))
-        nc.vector.quantize_mx(out=q_codes[:].bitcast(FP8X4), scales=q_scales[:], in_=q_bf[:].rearrange("p q j -> p (q j)"))
-
-        v_pool = sb.tile([P, POOL_PAGES * DV], I32, name="v_pool", align_bytes=64)
-        nc.sync.dma_start(
-            v_pool[:].rearrange("p (u e) -> p u e", u=POOL_PAGES),
-            v_words.rearrange("u p e r -> p u (e r)").bitcast(I32),
-        )
 
         def page_offsets(e):
             return offs_sb[:, e * PAGE // 16 : (e + 1) * PAGE // 16]
@@ -98,7 +108,6 @@ def tile_attend_pkv8_cap_kernel(tc, qT, k_words, k_scales, v_words, v_scales, vs
             nc.scalar.activation(ex[e][:], th[e][:, :PAGE], ACT.Exp, scale=CAP, accum_out=l_page[:, e : e + 1])
 
         for e in range(PAGES):
-            cols = slice(e * PAGE, (e + 1) * PAGE)
             nc.vector.tensor_copy(k_g[e][:], k_pool[:].bitcast(U32).indirect(page_offsets(e)))
             score = ps.tile([P, PAGE], F32, name=f"score{e}", tag=f"bank{e}")
             nc.tensor.matmul_mx(
@@ -106,7 +115,7 @@ def tile_attend_pkv8_cap_kernel(tc, qT, k_words, k_scales, v_words, v_scales, vs
                 lhsT=q_codes[:].bitcast(FP8X4),
                 lhsT_scale=q_scales[:],
                 rhs=k_g[e][:].bitcast(FP8X4),
-                rhs_scale=ks_g[:, cols],
+                rhs_scale=ks_plane[e // 2][:].bitcast(U8)[:, e % 2 * PAGE : (e % 2 + 1) * PAGE],
                 start=True,
                 stop=True,
             )
@@ -125,8 +134,13 @@ def tile_attend_pkv8_cap_kernel(tc, qT, k_words, k_scales, v_words, v_scales, vs
         w_codes = [sb.tile([P, NQ], U32, name=f"w_codes{e}", align_bytes=64) for e in range(PAGES)]
         w_scales = [sb.tile([P, NQ], U8, name=f"w_scales{e}", align_bytes=64) for e in range(PAGES)]
 
+        def page_parts(e):
+            return ((0, PAGE // 2), (PAGE // 2, PAGE)) if e == last else ((0, PAGE),)
+
         def weigh_page(e):
-            nc.vector.tensor_tensor(w_f32[e], vs_pool[:].indirect(page_offsets(e)), ex[e][:], ALU.mult)
+            for s0, s1 in page_parts(e):
+                listed = offs_sb[:, (e * PAGE + s0) // 16 : (e * PAGE + s1) // 16]
+                nc.vector.tensor_tensor(w_f32[e][:, s0:s1], vs_pool[:].indirect(listed), ex[e][:, s0:s1], ALU.mult)
 
         th_max = sb.tile([P, 1], F32, name="th_max")
         nc.vector.tensor_reduce(th_max[:], th[last][:], mybir.AxisListType.X, ALU.max)
@@ -136,14 +150,16 @@ def tile_attend_pkv8_cap_kernel(tc, qT, k_words, k_scales, v_words, v_scales, vs
             weigh_page(e)
 
         v_g = sb.tile([P, PAGES * DV], U32, name="v_g", tag=f"ex{last - 1}", align_bytes=64)
-        vsc_g = sb.tile([P, PAGES * DV], U8, name="vsc_g", tag=f"ex{last}", align_bytes=64)
         nc.vector.tensor_copy(v_g[:], v_pool[:].bitcast(U32).indirect(voffs_sb[:]))
-        nc.vector.tensor_copy(vsc_g[:], vsc_pool[:].bitcast(U8).indirect(voffs_sb[:]))
 
         for e in range(PAGES):
-            nc.scalar.activation(
-                w_row[e][:], w_f32[e].rearrange("q (p u j) -> q u p j", u=2, j=2), ACT.Copy, scale=exp_neg_m[:]
-            )
+            for s0, s1 in page_parts(e):
+                nc.scalar.activation(
+                    w_row[e][:, :, s0 // PACK : s1 // PACK, :],
+                    w_f32[e][:, s0:s1].rearrange("q (p u j) -> q u p j", u=2, j=2),
+                    ACT.Copy,
+                    scale=exp_neg_m[:],
+                )
             turned = ps.tile([P, 2, NQ], F32, name=f"turned{e}", tag=f"bank{e}")
             for u in range(2):
                 nc.tensor.transpose(
@@ -171,7 +187,7 @@ def tile_attend_pkv8_cap_kernel(tc, qT, k_words, k_scales, v_words, v_scales, vs
                 lhsT=w_codes[e][:].bitcast(FP8X4),
                 lhsT_scale=w_scales[e][:],
                 rhs=v_g[:, cols].bitcast(FP8X4),
-                rhs_scale=vsc_g[:, cols],
+                rhs_scale=vsc_plane[:].bitcast(U8)[:, cols],
                 start=(e == 0),
                 stop=(e == PAGES - 1),
             )

@@ -1,7 +1,6 @@
 from contextlib import ExitStack
 
 import concourse.mybir as mybir
-from concourse.masks import make_identity
 
 N, T, D, DV, NQ = 2048, 4096, 512, 128, 128
 PAGE = 512
@@ -45,19 +44,25 @@ def tile_attend_pkv8_cap_kernel(tc, qT, k_words, k_scales, v_words, v_scales, vs
         v_pool = sb.tile([P, POOL_PAGES * DV], I32, name="v_pool", align_bytes=64)
         ident = sb.tile([P, P], F32, name="ident")
 
-        make_identity(nc, ident[:])
-        for zeroed in (vsc_pool, ks_pool, ks_plane[0], ks_plane[1], vsc_plane):
+        nc.vector.memset(vsc_pool[:], 0)
+        nc.vector.memset(ks_pool[:], 0)
+        nc.vector.memset(ident[:], 0.0)
+        for zeroed in (ks_plane[0], ks_plane[1], vsc_plane):
             nc.vector.memset(zeroed[:], 0)
+        nc.gpsimd.affine_select(
+            out=ident[:], in_=ident[:], compare_op=ALU.not_equal, fill=1.0, base=0, pattern=[[-1, P]],
+            channel_multiplier=1,
+        )
 
-        nc.sync.dma_start(offs_sb[:], offs)
+        nc.scalar.dma_start(vs_cols[:], vs[0].rearrange("(p j) -> p j", p=P))
+        nc.scalar.dma_start(q_raw[:], qT[0].rearrange("(p j) q -> p j q", j=PACK))
         nc.sync.dma_start(voffs_sb[:], voffs)
         nc.sync.dma_start(
             vsc_pool[0:P:8, :].rearrange("f (u e) -> f u e", u=POOL_PAGES),
             v_scales.bitcast(I32).rearrange("u f e -> f u e"),
         )
-        nc.sync.dma_start(q_raw[:], qT[0].rearrange("(p j) q -> p j q", j=PACK))
+        nc.sync.dma_start(offs_sb[:], offs)
         nc.sync.dma_start(ks_pool[0:P:8, :], k_scales[0].bitcast(I32))
-        nc.sync.dma_start(vs_cols[:], vs[0].rearrange("(p j) -> p j", p=P))
         nc.sync.dma_start(k_pool[:], k_words[0].rearrange("p t r -> p (t r)").bitcast(I32))
 
         q_bf = sb.tile([P, NQ, PACK], BF16, name="q_bf", align_bytes=64)

@@ -125,10 +125,10 @@ def tile_attend_pkv8_cap_kernel(tc, qT, k_words, k_scales, v_words, v_scales, vs
                 stop=True,
             )
             nc.scalar.activation(th[e][:, :PAGE], score[:], ACT.Tanh, scale=1.0 / CAP)
-            if e < PAGES - 2:
-                exp_page(e)
-        exp_page(PAGES - 2)
-        exp_page(PAGES - 1)
+            if e == last - 1:
+                exp_page(0)
+        for e in range(1, PAGES):
+            exp_page(e)
 
         for e in range(last):
             nc.vector.tensor_reduce(th[last][:, PAGE + e : PAGE + e + 1], th[e][:], mybir.AxisListType.X, ALU.max)
@@ -184,7 +184,7 @@ def tile_attend_pkv8_cap_kernel(tc, qT, k_words, k_scales, v_words, v_scales, vs
         nc.scalar.activation(l_scaled[:], l_page[:], ACT.Copy, scale=exp_neg_m[:], accum_out=l_sum[:])
         nc.vector.reciprocal(l_inv[:], l_sum[:])
 
-        acc = ps.tile([P, DV], F32, name="acc", tag=f"bank{last}")
+        acc = ps.tile([P, DV], F32, name="acc", tag=f"bank{last - 1}")
         for e in range(PAGES):
             cols = slice(e * DV, (e + 1) * DV)
             nc.tensor.matmul_mx(

@@ -23,6 +23,7 @@ P = 128
 PACK = 4
 PAGES = N // PAGE
 POOL_PAGES = T // PAGE
+FUSED = 2
 
 
 def tile_attend_pkv8_cap_kernel(tc, qT, k_words, k_scales, v_words, v_scales, vs, offs, voffs, out):
@@ -101,16 +102,13 @@ def tile_attend_pkv8_cap_kernel(tc, qT, k_words, k_scales, v_words, v_scales, vs
         def page_offsets(e):
             return offs_sb[:, e * PAGE // 16 : (e + 1) * PAGE // 16]
 
-        k_g = [sb.tile([P, PAGE], U32, name=f"k_g{e}", align_bytes=64) for e in range(PAGES)]
+        k_g = [sb.tile([P, PAGE], U32, name=f"k_g{e}", tag=f"k_g{e}", align_bytes=64) for e in range(PAGES)]
         last = PAGES - 1
         th = [
             sb.tile([P, PAGE + (last if e == last else 0)], F32, name=f"th{e}", tag=f"th{e}", align_bytes=64) for e in range(PAGES)
         ]
         ex = [sb.tile([P, PAGE], F32, name=f"ex{e}", tag=f"ex{e}", align_bytes=64) for e in range(PAGES)]
         l_page = sb.tile([P, PAGES], F32, name="l_page")
-
-        def exp_page(e):
-            nc.scalar.activation(ex[e][:], th[e][:, :PAGE], ACT.Exp, scale=CAP, accum_out=l_page[:, e : e + 1])
 
         for e in range(PAGES):
             nc.vector.tensor_copy(k_g[e][:], k_pool[:].bitcast(U32).indirect(page_offsets(e)))
@@ -125,46 +123,44 @@ def tile_attend_pkv8_cap_kernel(tc, qT, k_words, k_scales, v_words, v_scales, vs
                 stop=True,
             )
             nc.scalar.activation(th[e][:, :PAGE], score[:], ACT.Tanh, scale=1.0 / CAP)
-            if e == last - 1:
-                exp_page(0)
-        for e in range(1, PAGES):
-            exp_page(e)
+        for e in range(PAGES):
+            nc.scalar.activation(ex[e][:], th[e][:, :PAGE], ACT.Exp, scale=CAP, accum_out=l_page[:, e : e + 1])
 
+        vs_late = sb.tile([P, PAGES - FUSED, PAGE], F32, name="vs_late", tag="k_g0", align_bytes=64)
+        nc.vector.tensor_copy(
+            vs_late[:].rearrange("q e s -> q (e s)"), vs_pool[:].indirect(offs_sb[:, FUSED * PAGE // 16 :])
+        )
         for e in range(last):
             nc.vector.tensor_reduce(th[last][:, PAGE + e : PAGE + e + 1], th[e][:], mybir.AxisListType.X, ALU.max)
+        th_max = sb.tile([P, 1], F32, name="th_max")
+        nc.vector.tensor_reduce(th_max[:], th[last][:], mybir.AxisListType.X, ALU.max)
+        exp_neg_m = sb.tile([P, 1], F32, name="exp_neg_m")
+        nc.scalar.activation(exp_neg_m[:], th_max[:], ACT.Exp, scale=-CAP)
 
-        w_f32 = [sb.tile([P, PAGE], F32, name=f"w_f32{e}", align_bytes=64)[:] for e in range(PAGES)]
         w_row = [sb.tile([P, 2, P, 2], BF16, name=f"w_row{e}", align_bytes=64) for e in range(PAGES)]
         w_bf = [sb.tile([P, NQ, PACK], BF16, name=f"w_bf{e}", align_bytes=64) for e in range(PAGES)]
         w_codes = [sb.tile([P, NQ], U32, name=f"w_codes{e}", align_bytes=64) for e in range(PAGES)]
         w_scales = [sb.tile([P, NQ], U8, name=f"w_scales{e}", align_bytes=64) for e in range(PAGES)]
 
-        def page_parts(e):
-            return ((0, PAGE // 2), (PAGE // 2, PAGE)) if e == last else ((0, PAGE),)
+        def by_pairs(row):
+            return row.rearrange("q (p u j) -> q u p j", u=2, j=2)
 
-        def weigh_page(e):
-            for s0, s1 in page_parts(e):
-                listed = offs_sb[:, (e * PAGE + s0) // 16 : (e * PAGE + s1) // 16]
-                nc.vector.tensor_tensor(w_f32[e][:, s0:s1], vs_pool[:].indirect(listed), ex[e][:, s0:s1], ALU.mult)
-
-        th_max = sb.tile([P, 1], F32, name="th_max")
-        nc.vector.tensor_reduce(th_max[:], th[last][:], mybir.AxisListType.X, ALU.max)
-        exp_neg_m = sb.tile([P, 1], F32, name="exp_neg_m")
-        nc.scalar.activation(exp_neg_m[:], th_max[:], ACT.Exp, scale=-CAP)
-        for e in range(PAGES):
-            weigh_page(e)
+        for e in range(FUSED):
+            w_f32 = sb.tile([P, PAGE], F32, name=f"w_f32{e}", align_bytes=64)
+            nc.vector.tensor_tensor(w_f32[:], vs_pool[:].indirect(page_offsets(e)), ex[e][:], ALU.mult)
+            nc.scalar.activation(w_row[e][:], by_pairs(w_f32[:]), ACT.Copy, scale=exp_neg_m[:])
+        for e in range(FUSED, PAGES):
+            for u in range(2):
+                nc.vector.scalar_tensor_tensor(
+                    w_row[e][:, u], by_pairs(ex[e][:])[:, u], exp_neg_m[:], by_pairs(vs_late[:, e - FUSED, :])[:, u],
+                    ALU.mult, ALU.mult,
+                )
 
         v_g = sb.tile([P, PAGES * DV], U32, name="v_g", tag=f"ex{last - 1}", align_bytes=64)
         nc.vector.tensor_copy(v_g[:], v_pool[:].bitcast(U32).indirect(voffs_sb[:]))
 
-        for e in range(PAGES):
-            for s0, s1 in page_parts(e):
-                nc.scalar.activation(
-                    w_row[e][:, :, s0 // PACK : s1 // PACK, :],
-                    w_f32[e][:, s0:s1].rearrange("q (p u j) -> q u p j", u=2, j=2),
-                    ACT.Copy,
-                    scale=exp_neg_m[:],
-                )
+        order = (0, 2, 1, 3)
+        for e in order:
             turned = ps.tile([P, 2, NQ], F32, name=f"turned{e}", tag=f"bank{e}")
             for u in range(2):
                 nc.tensor.transpose(
@@ -185,7 +181,7 @@ def tile_attend_pkv8_cap_kernel(tc, qT, k_words, k_scales, v_words, v_scales, vs
         nc.vector.reciprocal(l_inv[:], l_sum[:])
 
         acc = ps.tile([P, DV], F32, name="acc", tag=f"bank{last - 1}")
-        for e in range(PAGES):
+        for e in order:
             cols = slice(e * DV, (e + 1) * DV)
             nc.tensor.matmul_mx(
                 out=acc[:],

@@ -104,10 +104,12 @@ def tile_attend_pkv8_cap_kernel(tc, qT, k_words, k_scales, v_words, v_scales, vs
 
         k_g = [sb.tile([P, PAGE], U32, name=f"k_g{e}", tag=f"k_g{e}", align_bytes=64) for e in range(PAGES)]
         last = PAGES - 1
-        th = [
-            sb.tile([P, PAGE + (last if e == last else 0)], F32, name=f"th{e}", tag=f"th{e}", align_bytes=64) for e in range(PAGES)
+        th_all = sb.tile([P, N], F32, name="th_all", align_bytes=64)
+        th = [th_all[:, e * PAGE : (e + 1) * PAGE] for e in range(PAGES)]
+        ex = [
+            sb.tile([P, PAGE], F32, name=f"ex{e}", tag=f"k_g{last - e}" if e < FUSED else f"ex{e}", align_bytes=64)
+            for e in range(PAGES)
         ]
-        ex = [sb.tile([P, PAGE], F32, name=f"ex{e}", tag=f"ex{e}", align_bytes=64) for e in range(PAGES)]
         l_page = sb.tile([P, PAGES], F32, name="l_page")
 
         for e in range(PAGES):
@@ -122,18 +124,14 @@ def tile_attend_pkv8_cap_kernel(tc, qT, k_words, k_scales, v_words, v_scales, vs
                 start=True,
                 stop=True,
             )
-            nc.scalar.activation(th[e][:, :PAGE], score[:], ACT.Tanh, scale=1.0 / CAP)
+            nc.scalar.activation(th[e], score[:], ACT.Tanh, scale=1.0 / CAP)
         for e in range(PAGES):
-            nc.scalar.activation(ex[e][:], th[e][:, :PAGE], ACT.Exp, scale=CAP, accum_out=l_page[:, e : e + 1])
+            nc.scalar.activation(ex[e][:], th[e], ACT.Exp, scale=CAP, accum_out=l_page[:, e : e + 1])
 
-        vs_late = sb.tile([P, PAGES - FUSED, PAGE], F32, name="vs_late", tag="k_g0", align_bytes=64)
-        nc.vector.tensor_copy(
-            vs_late[:].rearrange("q e s -> q (e s)"), vs_pool[:].indirect(offs_sb[:, FUSED * PAGE // 16 :])
-        )
-        for e in range(last):
-            nc.vector.tensor_reduce(th[last][:, PAGE + e : PAGE + e + 1], th[e][:], mybir.AxisListType.X, ALU.max)
+        vs_early = sb.tile([P, FUSED * PAGE], F32, name="vs_early", tag="k_g0", align_bytes=64)
+        nc.vector.tensor_copy(vs_early[:], vs_pool[:].indirect(offs_sb[:, : FUSED * PAGE // 16]))
         th_max = sb.tile([P, 1], F32, name="th_max")
-        nc.vector.tensor_reduce(th_max[:], th[last][:], mybir.AxisListType.X, ALU.max)
+        nc.vector.tensor_reduce(th_max[:], th_all[:], mybir.AxisListType.X, ALU.max)
         exp_neg_m = sb.tile([P, 1], F32, name="exp_neg_m")
         nc.scalar.activation(exp_neg_m[:], th_max[:], ACT.Exp, scale=-CAP)
 
@@ -147,8 +145,12 @@ def tile_attend_pkv8_cap_kernel(tc, qT, k_words, k_scales, v_words, v_scales, vs
 
         for e in range(FUSED):
             w_f32 = sb.tile([P, PAGE], F32, name=f"w_f32{e}", align_bytes=64)
-            nc.vector.tensor_tensor(w_f32[:], vs_pool[:].indirect(page_offsets(e)), ex[e][:], ALU.mult)
+            nc.gpsimd.tensor_tensor(w_f32[:], vs_early[:, e * PAGE : (e + 1) * PAGE], ex[e][:], ALU.mult)
             nc.scalar.activation(w_row[e][:], by_pairs(w_f32[:]), ACT.Copy, scale=exp_neg_m[:])
+        vs_late = sb.tile([P, PAGES - FUSED, PAGE], F32, name="vs_late", tag=f"k_g{last}", align_bytes=64)
+        nc.vector.tensor_copy(
+            vs_late[:].rearrange("q e s -> q (e s)"), vs_pool[:].indirect(offs_sb[:, FUSED * PAGE // 16 :])
+        )
         for e in range(FUSED, PAGES):
             for u in range(2):
                 nc.vector.scalar_tensor_tensor(
@@ -176,7 +178,7 @@ def tile_attend_pkv8_cap_kernel(tc, qT, k_words, k_scales, v_words, v_scales, vs
 
         l_scaled = sb.tile([P, PAGES], F32, name="l_scaled")
         l_sum = sb.tile([P, 1], F32, name="l_sum")
-        l_inv = sb.tile([P, 1], F32, name="l_inv", tag="ex0", align_bytes=64)
+        l_inv = sb.tile([P, 1], F32, name="l_inv", tag=f"ex{last}", align_bytes=64)
         nc.scalar.activation(l_scaled[:], l_page[:], ACT.Copy, scale=exp_neg_m[:], accum_out=l_sum[:])
         nc.vector.reciprocal(l_inv[:], l_sum[:])
 

@@ -104,14 +104,18 @@ def tile_attend_pkv8_cap_kernel(tc, qT, k_words, k_scales, v_words, v_scales, vs
 
         k_g = [sb.tile([P, PAGE], U32, name=f"k_g{e}", tag=f"k_g{e}", align_bytes=64) for e in range(PAGES)]
         last = PAGES - 1
-        th_all = sb.tile([P, N], F32, name="th_all", align_bytes=64)
+        th_all = sb.tile([P, N + 1], F32, name="th_all", tag="th_all", align_bytes=64)
         th = [th_all[:, e * PAGE : (e + 1) * PAGE] for e in range(PAGES)]
         ex = [
-            sb.tile([P, PAGE], F32, name=f"ex{e}", tag=f"k_g{last - e}" if e < FUSED else f"ex{e}", align_bytes=64)
+            sb.tile([P, PAGE], F32, name=f"ex{e}", tag=f"k_g{e + 2}" if e < 2 else f"ex{e}", align_bytes=64)
             for e in range(PAGES)
         ]
         l_page = sb.tile([P, PAGES], F32, name="l_page")
+        w_f32 = [sb.tile([P, PAGE], F32, name=f"w_f32{e}", tag=f"w_f32{e}", align_bytes=64) for e in range(PAGES)]
+        th_max = sb.tile([P, 1], F32, name="th_max")
+        exp_neg_m = sb.tile([P, 1], F32, name="exp_neg_m")
 
+        scores = []
         for e in range(PAGES):
             nc.vector.tensor_copy(k_g[e][:], k_pool[:].bitcast(U32).indirect(page_offsets(e)))
             score = ps.tile([P, PAGE], F32, name=f"score{e}", tag=f"bank{e}")
@@ -124,19 +128,36 @@ def tile_attend_pkv8_cap_kernel(tc, qT, k_words, k_scales, v_words, v_scales, vs
                 start=True,
                 stop=True,
             )
-            nc.scalar.activation(th[e], score[:], ACT.Tanh, scale=1.0 / CAP)
-        for e in range(PAGES):
+            scores.append(score)
+
+        def cap(e):
+            nc.scalar.activation(th[e], scores[e][:], ACT.Tanh, scale=1.0 / CAP)
+
+        def exponentiate(e):
             nc.scalar.activation(ex[e][:], th[e], ACT.Exp, scale=CAP, accum_out=l_page[:, e : e + 1])
 
-        vs_early = sb.tile([P, FUSED * PAGE], F32, name="vs_early", tag="k_g0", align_bytes=64)
-        nc.vector.tensor_copy(vs_early[:], vs_pool[:].indirect(offs_sb[:, : FUSED * PAGE // 16]))
-        th_max = sb.tile([P, 1], F32, name="th_max")
-        nc.vector.tensor_reduce(th_max[:], th_all[:], mybir.AxisListType.X, ALU.max)
-        exp_neg_m = sb.tile([P, 1], F32, name="exp_neg_m")
-        nc.scalar.activation(exp_neg_m[:], th_max[:], ACT.Exp, scale=-CAP)
+        def weigh(e):
+            nc.vector.tensor_tensor(w_f32[e][:], vs_pool[:].indirect(page_offsets(e)), ex[e][:], ALU.mult)
 
-        w_row = [sb.tile([P, 2, P, 2], BF16, name=f"w_row{e}", align_bytes=64) for e in range(PAGES)]
-        w_bf = [sb.tile([P, NQ, PACK], BF16, name=f"w_bf{e}", align_bytes=64) for e in range(PAGES)]
+        for e in range(last):
+            cap(e)
+        exponentiate(0)
+        cap(last)
+        nc.vector.tensor_reduce(th_all[:, N:], th_all[:, :half], mybir.AxisListType.X, ALU.max)
+        weigh(0)
+        nc.vector.tensor_reduce(th_max[:], th_all[:, half:], mybir.AxisListType.X, ALU.max)
+        for e in range(1, last):
+            exponentiate(e)
+        nc.scalar.activation(exp_neg_m[:], th_max[:], ACT.Exp, scale=-CAP)
+        exponentiate(last)
+        for e in range(1, PAGES):
+            weigh(e)
+
+        w_row = [
+            sb.tile([P, 2, P, 2], BF16, name=f"w_row{e}", tag="th_all" if e == FUSED else f"w_row{e}", align_bytes=64)
+            for e in range(PAGES)
+        ]
+        w_bf = [sb.tile([P, NQ, PACK], BF16, name=f"w_bf{e}", tag=f"w_bf{e}", align_bytes=64) for e in range(PAGES)]
         w_codes = [sb.tile([P, NQ], U32, name=f"w_codes{e}", align_bytes=64) for e in range(PAGES)]
         w_scales = [sb.tile([P, NQ], U8, name=f"w_scales{e}", align_bytes=64) for e in range(PAGES)]
 
@@ -144,24 +165,13 @@ def tile_attend_pkv8_cap_kernel(tc, qT, k_words, k_scales, v_words, v_scales, vs
             return row.rearrange("q (p u j) -> q u p j", u=2, j=2)
 
         for e in range(FUSED):
-            w_f32 = sb.tile([P, PAGE], F32, name=f"w_f32{e}", align_bytes=64)
-            nc.gpsimd.tensor_tensor(w_f32[:], vs_early[:, e * PAGE : (e + 1) * PAGE], ex[e][:], ALU.mult)
-            nc.scalar.activation(w_row[e][:], by_pairs(w_f32[:]), ACT.Copy, scale=exp_neg_m[:])
-        vs_late = sb.tile([P, PAGES - FUSED, PAGE], F32, name="vs_late", tag=f"k_g{last}", align_bytes=64)
-        nc.vector.tensor_copy(
-            vs_late[:].rearrange("q e s -> q (e s)"), vs_pool[:].indirect(offs_sb[:, FUSED * PAGE // 16 :])
-        )
+            nc.scalar.activation(w_row[e][:], by_pairs(w_f32[e][:]), ACT.Copy, scale=exp_neg_m[:])
         for e in range(FUSED, PAGES):
-            for u in range(2):
-                nc.vector.scalar_tensor_tensor(
-                    w_row[e][:, u], by_pairs(ex[e][:])[:, u], exp_neg_m[:], by_pairs(vs_late[:, e - FUSED, :])[:, u],
-                    ALU.mult, ALU.mult,
-                )
-
-        v_g = sb.tile([P, PAGES * DV], U32, name="v_g", tag=f"ex{last - 1}", align_bytes=64)
+            nc.vector.tensor_scalar(w_row[e][:], by_pairs(w_f32[e][:]), exp_neg_m[:], None, ALU.mult)
+        v_g = sb.tile([P, PAGES * DV], U32, name="v_g", tag=f"w_f32{FUSED}", align_bytes=64)
         nc.vector.tensor_copy(v_g[:], v_pool[:].bitcast(U32).indirect(voffs_sb[:]))
 
-        order = (0, 2, 1, 3)
+        order = (0, 1, 2, 3)
         for e in order:
             turned = ps.tile([P, 2, NQ], F32, name=f"turned{e}", tag=f"bank{e}")
             for u in range(2):
@@ -178,7 +188,7 @@ def tile_attend_pkv8_cap_kernel(tc, qT, k_words, k_scales, v_words, v_scales, vs
 
         l_scaled = sb.tile([P, PAGES], F32, name="l_scaled")
         l_sum = sb.tile([P, 1], F32, name="l_sum")
-        l_inv = sb.tile([P, 1], F32, name="l_inv", tag=f"ex{last}", align_bytes=64)
+        l_inv = sb.tile([P, 1], F32, name="l_inv", tag="w_bf1", align_bytes=64)
         nc.scalar.activation(l_scaled[:], l_page[:], ACT.Copy, scale=exp_neg_m[:], accum_out=l_sum[:])
         nc.vector.reciprocal(l_inv[:], l_sum[:])
 

@@ -104,7 +104,7 @@ def tile_attend_pkv8_cap_kernel(tc, qT, k_words, k_scales, v_words, v_scales, vs
 
         k_g = [sb.tile([P, PAGE], U32, name=f"k_g{e}", tag=f"k_g{e}", align_bytes=64) for e in range(PAGES)]
         last = PAGES - 1
-        th_all = sb.tile([P, N + 1], F32, name="th_all", tag="th_all", align_bytes=64)
+        th_all = sb.tile([P, N + last], F32, name="th_all", tag="th_all", align_bytes=64)
         th = [th_all[:, e * PAGE : (e + 1) * PAGE] for e in range(PAGES)]
         ex = [
             sb.tile([P, PAGE], F32, name=f"ex{e}", tag=f"k_g{e + 2}" if e < 2 else f"ex{e}", align_bytes=64)
@@ -118,20 +118,25 @@ def tile_attend_pkv8_cap_kernel(tc, qT, k_words, k_scales, v_words, v_scales, vs
         scores = []
         for e in range(PAGES):
             nc.vector.tensor_copy(k_g[e][:], k_pool[:].bitcast(U32).indirect(page_offsets(e)))
-            score = ps.tile([P, PAGE], F32, name=f"score{e}", tag=f"bank{e}")
-            nc.tensor.matmul_mx(
-                out=score[:],
-                lhsT=q_codes[:].bitcast(FP8X4),
-                lhsT_scale=q_scales[:],
-                rhs=k_g[e][:].bitcast(FP8X4),
-                rhs_scale=ks_plane[e // 2][:].bitcast(U8)[:, e % 2 * PAGE : (e % 2 + 1) * PAGE],
-                start=True,
-                stop=True,
-            )
-            scores.append(score)
+            width = PAGE // 2 if e == 0 else PAGE
+            parts = []
+            for c in range(0, PAGE, width):
+                score = ps.tile([P, width], F32, name=f"score{e}_{c}", tag=f"bank{e}" if c == 0 else "spread0")
+                nc.tensor.matmul_mx(
+                    out=score[:],
+                    lhsT=q_codes[:].bitcast(FP8X4),
+                    lhsT_scale=q_scales[:],
+                    rhs=k_g[e][:, c : c + width].bitcast(FP8X4),
+                    rhs_scale=ks_plane[e // 2][:].bitcast(U8)[:, e % 2 * PAGE + c : e % 2 * PAGE + c + width],
+                    start=True,
+                    stop=True,
+                )
+                parts.append((c, width, score))
+            scores.append(parts)
 
         def cap(e):
-            nc.scalar.activation(th[e], scores[e][:], ACT.Tanh, scale=1.0 / CAP)
+            for c, width, score in scores[e]:
+                nc.scalar.activation(th[e][:, c : c + width], score[:], ACT.Tanh, scale=1.0 / CAP)
 
         def exponentiate(e):
             nc.scalar.activation(ex[e][:], th[e], ACT.Exp, scale=CAP, accum_out=l_page[:, e : e + 1])
@@ -143,13 +148,13 @@ def tile_attend_pkv8_cap_kernel(tc, qT, k_words, k_scales, v_words, v_scales, vs
             cap(e)
         exponentiate(0)
         cap(last)
-        nc.vector.tensor_reduce(th_all[:, N:], th_all[:, :half], mybir.AxisListType.X, ALU.max)
+        for e in range(last):
+            nc.vector.tensor_reduce(th_all[:, N + e : N + e + 1], th[e], mybir.AxisListType.X, ALU.max)
         weigh(0)
-        nc.vector.tensor_reduce(th_max[:], th_all[:, half:], mybir.AxisListType.X, ALU.max)
-        for e in range(1, last):
+        nc.vector.tensor_reduce(th_max[:], th_all[:, last * PAGE :], mybir.AxisListType.X, ALU.max)
+        for e in range(1, PAGES):
             exponentiate(e)
         nc.scalar.activation(exp_neg_m[:], th_max[:], ACT.Exp, scale=-CAP)
-        exponentiate(last)
         for e in range(1, PAGES):
             weigh(e)
 
@@ -166,8 +171,10 @@ def tile_attend_pkv8_cap_kernel(tc, qT, k_words, k_scales, v_words, v_scales, vs
 
         for e in range(FUSED):
             nc.scalar.activation(w_row[e][:], by_pairs(w_f32[e][:]), ACT.Copy, scale=exp_neg_m[:])
-        for e in range(FUSED, PAGES):
+        for e in range(FUSED, last):
             nc.vector.tensor_scalar(w_row[e][:], by_pairs(w_f32[e][:]), exp_neg_m[:], None, ALU.mult)
+        for u in range(2):
+            nc.vector.tensor_scalar(w_row[last][:, u], by_pairs(w_f32[last][:])[:, u], exp_neg_m[:], None, ALU.mult)
         v_g = sb.tile([P, PAGES * DV], U32, name="v_g", tag=f"w_f32{FUSED}", align_bytes=64)
         nc.vector.tensor_copy(v_g[:], v_pool[:].bitcast(U32).indirect(voffs_sb[:]))
 

@@ -23,7 +23,6 @@ P = 128
 PACK = 4
 PAGES = N // PAGE
 POOL_PAGES = T // PAGE
-FUSED = 2
 
 
 def tile_attend_pkv8_cap_kernel(tc, qT, k_words, k_scales, v_words, v_scales, vs, offs, voffs, out):
@@ -152,16 +151,13 @@ def tile_attend_pkv8_cap_kernel(tc, qT, k_words, k_scales, v_words, v_scales, vs
             nc.vector.tensor_reduce(th_all[:, N + e : N + e + 1], th[e], mybir.AxisListType.X, ALU.max)
         weigh(0)
         nc.vector.tensor_reduce(th_max[:], th_all[:, last * PAGE :], mybir.AxisListType.X, ALU.max)
-        for e in range(1, PAGES):
+        for e in range(1, last):
             exponentiate(e)
-        nc.scalar.activation(exp_neg_m[:], th_max[:], ACT.Exp, scale=-CAP)
-        for e in range(1, PAGES):
             weigh(e)
+        nc.scalar.activation(exp_neg_m[:], th_max[:], ACT.Exp, scale=-CAP)
+        exponentiate(last)
 
-        w_row = [
-            sb.tile([P, 2, P, 2], BF16, name=f"w_row{e}", tag="th_all" if e == FUSED else f"w_row{e}", align_bytes=64)
-            for e in range(PAGES)
-        ]
+        w_row = [sb.tile([P, 2, P, 2], BF16, name=f"w_row{e}", align_bytes=64) for e in range(PAGES)]
         w_bf = [sb.tile([P, NQ, PACK], BF16, name=f"w_bf{e}", tag=f"w_bf{e}", align_bytes=64) for e in range(PAGES)]
         w_codes = [sb.tile([P, NQ], U32, name=f"w_codes{e}", align_bytes=64) for e in range(PAGES)]
         w_scales = [sb.tile([P, NQ], U8, name=f"w_scales{e}", align_bytes=64) for e in range(PAGES)]
@@ -169,18 +165,32 @@ def tile_attend_pkv8_cap_kernel(tc, qT, k_words, k_scales, v_words, v_scales, vs
         def by_pairs(row):
             return row.rearrange("q (p u j) -> q u p j", u=2, j=2)
 
-        for e in range(FUSED):
+        nc.vector.tensor_scalar(w_row[0][:], by_pairs(w_f32[0][:]), exp_neg_m[:], None, ALU.mult)
+        for e in range(1, last):
             nc.scalar.activation(w_row[e][:], by_pairs(w_f32[e][:]), ACT.Copy, scale=exp_neg_m[:])
-        for e in range(FUSED, last):
-            nc.vector.tensor_scalar(w_row[e][:], by_pairs(w_f32[e][:]), exp_neg_m[:], None, ALU.mult)
-        for u in range(2):
-            nc.vector.tensor_scalar(w_row[last][:, u], by_pairs(w_f32[last][:])[:, u], exp_neg_m[:], None, ALU.mult)
-        v_g = sb.tile([P, PAGES * DV], U32, name="v_g", tag=f"w_f32{FUSED}", align_bytes=64)
-        nc.vector.tensor_copy(v_g[:], v_pool[:].bitcast(U32).indirect(voffs_sb[:]))
+        for h in range(2):
+            slots = slice(h * PAGE // 2, (h + 1) * PAGE // 2)
+            offsets = offs_sb[:, (last * PAGE + slots.start) // 16 : (last * PAGE + slots.stop) // 16]
+            nc.vector.tensor_tensor(w_f32[last][:, slots], vs_pool[:].indirect(offsets), ex[last][:, slots], ALU.mult)
+        for h in range(2):
+            words = slice(h * P // 2, (h + 1) * P // 2)
+            nc.vector.tensor_scalar(
+                w_row[last][:, :, words, :], by_pairs(w_f32[last][:])[:, :, words, :], exp_neg_m[:], None, ALU.mult
+            )
+        v_g = [
+            sb.tile([P, 2 * DV], U32, name=f"v_g{h}", tag=(f"ex{last}", "w_bf0")[h], align_bytes=64) for h in range(2)
+        ]
+
+        def gather_values(h):
+            nc.vector.tensor_copy(
+                v_g[h][:], v_pool[:].bitcast(U32).indirect(voffs_sb[:, h * 2 * DV // 16 : (h + 1) * 2 * DV // 16])
+            )
+
+        gather_values(0)
 
         order = (0, 1, 2, 3)
         for e in order:
-            turned = ps.tile([P, 2, NQ], F32, name=f"turned{e}", tag=f"bank{e}")
+            turned = ps.tile([P, 2, NQ], F32, name=f"turned{e}", tag=f"bank{e % last}")
             for u in range(2):
                 nc.tensor.transpose(
                     turned[:, u, :], w_row[e][:, u].rearrange("q p j -> q (p j)").bitcast(F32), ident[:]
@@ -192,6 +202,8 @@ def tile_attend_pkv8_cap_kernel(tc, qT, k_words, k_scales, v_words, v_scales, vs
             nc.vector.quantize_mx(
                 out=w_codes[e][:].bitcast(FP8X4), scales=w_scales[e][:], in_=w_bf[e][:].rearrange("p q t -> p (q t)")
             )
+            if e == 1:
+                gather_values(1)
 
         l_scaled = sb.tile([P, PAGES], F32, name="l_scaled")
         l_sum = sb.tile([P, 1], F32, name="l_sum")
@@ -206,7 +218,7 @@ def tile_attend_pkv8_cap_kernel(tc, qT, k_words, k_scales, v_words, v_scales, vs
                 out=acc[:],
                 lhsT=w_codes[e][:].bitcast(FP8X4),
                 lhsT_scale=w_scales[e][:],
-                rhs=v_g[:, cols].bitcast(FP8X4),
+                rhs=v_g[e // 2][:, e % 2 * DV : (e % 2 + 1) * DV].bitcast(FP8X4),
                 rhs_scale=vsc_plane[:].bitcast(U8)[:, cols],
                 start=(e == 0),
                 stop=(e == PAGES - 1),

@@ -32,38 +32,42 @@ def tile_attend_pkv8_cap_kernel(tc, qT, k_words, k_scales, v_words, v_scales, vs
         ps = ctx.enter_context(tc.psum_pool(name="ps", bufs=1))
 
         half = N // 2
+        last = PAGES - 1
+        vs_row = P - 1
         offs_sb = sb.tile([P, N // 16], U16, name="offs_sb")
         voffs_sb = sb.tile([P, PAGES * DV // 16], U16, name="voffs_sb")
-        ks_pool = sb.tile([P, T // 4], I32, name="ks_pool", align_bytes=64)
-        vsc_pool = sb.tile([P, POOL_PAGES * DV // 4], I32, name="vsc_pool", align_bytes=64)
+        ks_pool = sb.tile([P, T // 4], I32, name="ks_pool", tag="ks_pool", align_bytes=64)
+        vsc_pool = sb.tile([P, POOL_PAGES * DV // 4], I32, name="vsc_pool", tag="vsc_pool", align_bytes=64)
         ks_plane = [sb.tile([P, half // 4], I32, name=f"ks_plane{h}", align_bytes=64) for h in range(2)]
         vsc_plane = sb.tile([P, PAGES * DV // 4], I32, name="vsc_plane", align_bytes=64)
         q_raw = sb.tile([P, PACK, NQ], F32, name="q_raw")
-        vs_cols = sb.tile([P, T // P], F32, name="vs_cols")
+        vs_pool = sb.tile([P, T], F32, name="vs_pool", align_bytes=64)
         k_pool = sb.tile([P, T], I32, name="k_pool", align_bytes=64)
-        v_pool = sb.tile([P, POOL_PAGES * DV], I32, name="v_pool", align_bytes=64)
         ident = sb.tile([P, P], F32, name="ident")
 
-        nc.vector.memset(vsc_pool[:], 0)
         nc.vector.memset(ks_pool[:], 0)
-        nc.vector.memset(ident[:], 0.0)
+        nc.vector.memset(vsc_pool[:], 0)
+        nc.vector.memset(vs_pool[0:vs_row, :], 0.0)
         for zeroed in (ks_plane[0], ks_plane[1], vsc_plane):
             nc.vector.memset(zeroed[:], 0)
+        nc.gpsimd.memset(ident[:], 0.0)
         nc.gpsimd.affine_select(
             out=ident[:], in_=ident[:], compare_op=ALU.not_equal, fill=1.0, base=0, pattern=[[-1, P]],
             channel_multiplier=1,
         )
 
-        nc.scalar.dma_start(vs_cols[:], vs[0].rearrange("(p j) -> p j", p=P))
-        nc.scalar.dma_start(q_raw[:], qT[0].rearrange("(p j) q -> p j q", j=PACK))
+        nc.sync.dma_start(offs_sb[:], offs)
         nc.sync.dma_start(voffs_sb[:], voffs)
+        nc.scalar.dma_start(vs_pool[vs_row:P, :], vs[0:1, :])
+        nc.scalar.dma_start(q_raw[:], qT[0].rearrange("(p j) q -> p j q", j=PACK))
         nc.sync.dma_start(
+            k_pool[:], k_words[0].rearrange("p t r -> p (t r)").bitcast(I32), max_dma_last_dim=4096
+        )
+        nc.scalar.dma_start(ks_pool[0:P:8, :], k_scales[0].bitcast(I32))
+        nc.scalar.dma_start(
             vsc_pool[0:P:8, :].rearrange("f (u e) -> f u e", u=POOL_PAGES),
             v_scales.bitcast(I32).rearrange("u f e -> f u e"),
         )
-        nc.sync.dma_start(offs_sb[:], offs)
-        nc.sync.dma_start(ks_pool[0:P:8, :], k_scales[0].bitcast(I32))
-        nc.sync.dma_start(k_pool[:], k_words[0].rearrange("p t r -> p (t r)").bitcast(I32))
 
         q_bf = sb.tile([P, NQ, PACK], BF16, name="q_bf", align_bytes=64)
         q_codes = sb.tile([P, NQ], U32, name="q_codes", align_bytes=64)
@@ -74,8 +78,9 @@ def tile_attend_pkv8_cap_kernel(tc, qT, k_words, k_scales, v_words, v_scales, vs
             for g in range(4):
                 nc.sync.dma_start(plane[g:P:32, :], gathered[8 * g : P : 32, :].bitcast(I32))
 
-        vsc_g = sb.tile([P, PAGES * DV], U8, name="vsc_g", align_bytes=64)
-        nc.vector.tensor_copy(vsc_g[:], vsc_pool[:].bitcast(U8).indirect(voffs_sb[:]))
+        def page_offsets(e):
+            return offs_sb[:, e * PAGE // 16 : (e + 1) * PAGE // 16]
+
         for h in range(2):
             ks_g = sb.tile([P, half], U8, name=f"ks_g{h}", align_bytes=64)
             nc.vector.tensor_copy(
@@ -83,49 +88,59 @@ def tile_attend_pkv8_cap_kernel(tc, qT, k_words, k_scales, v_words, v_scales, vs
             )
             place_scale_rows(ks_plane[h], ks_g)
         nc.vector.quantize_mx(out=q_codes[:].bitcast(FP8X4), scales=q_scales[:], in_=q_bf[:].rearrange("p q j -> p (q j)"))
+        vsc_g = sb.tile([P, PAGES * DV], U8, name="vsc_g", align_bytes=64)
+        nc.vector.tensor_copy(vsc_g[:], vsc_pool[:].bitcast(U8).indirect(voffs_sb[:]))
+        v_pool = sb.tile([P, POOL_PAGES * DV], I32, name="v_pool", tag="ks_pool", align_bytes=64)
         nc.sync.dma_start(
             v_pool[:].rearrange("p (u e) -> p u e", u=POOL_PAGES),
             v_words.rearrange("u p e r -> p u (e r)").bitcast(I32),
         )
         place_scale_rows(vsc_plane, vsc_g)
 
-        vs_pool = sb.tile([P, T], F32, name="vs_pool", align_bytes=64)
-        vs_runs = vs_pool[:].rearrange("q (p b t) -> q b p t", p=P, t=PACK)
-        for b in range(T // P // PACK):
-            spread = ps.tile([P, PACK, P], F32, name=f"spread{b}", tag=f"spread{b % 4}")
-            for t in range(PACK):
-                j = PACK * b + t
-                nc.tensor.transpose(spread[:, t, :], vs_cols[:, j : j + 1].to_broadcast([P, P]), ident[:])
-            nc.scalar.activation(vs_runs[:, b], spread[:].rearrange("q t p -> q p t"), ACT.Copy)
+        vs_cols = []
+        for e in range(PAGES):
+            vs_g = sb.tile([P, PAGE], F32, name=f"vs_g{e}", align_bytes=64)
+            nc.scalar.activation(vs_g[:], vs_pool[:].indirect(page_offsets(e)), ACT.Copy)
+            upright = ps.tile([P, PACK, P], F32, name=f"upright{e}", tag=("score2", "score1", "score0b", "score0")[e])
+            for j in range(PACK):
+                nc.tensor.transpose(upright[:, j, :], vs_g[:, j * P : (j + 1) * P], ident[:])
+            cols = sb.tile([P, PACK], F32, name=f"vs_cols{e}")
+            nc.scalar.copy(cols[:], upright[:, :, vs_row])
+            vs_cols.append(cols)
 
-        def page_offsets(e):
-            return offs_sb[:, e * PAGE // 16 : (e + 1) * PAGE // 16]
+        def spread(e, bank):
+            rows = ps.tile([P, PACK, P], F32, name=f"vs_rows{e}", tag=bank)
+            for j in range(PACK):
+                nc.tensor.transpose(rows[:, j, :], vs_cols[e][:, j : j + 1].to_broadcast([P, P]), ident[:])
+            return rows[:].rearrange("q j p -> q (j p)")
 
-        k_g = [sb.tile([P, PAGE], U32, name=f"k_g{e}", tag=f"k_g{e}", align_bytes=64) for e in range(PAGES)]
-        last = PAGES - 1
-        th_all = sb.tile([P, N + last], F32, name="th_all", tag="th_all", align_bytes=64)
-        th = [th_all[:, e * PAGE : (e + 1) * PAGE] for e in range(PAGES)]
-        ex = [
-            sb.tile([P, PAGE], F32, name=f"ex{e}", tag=f"k_g{e + 2}" if e < 2 else f"ex{e}", align_bytes=64)
+        vs_rows = [spread(0, "early")]
+
+        k_g = sb.tile([P, N], U32, name="k_g", tag="vsc_pool", align_bytes=64)
+        th = [
+            sb.tile([P, PAGE + (last if e == last else 0)], F32, name=f"th{e}", tag=f"th{e}", align_bytes=64)
             for e in range(PAGES)
         ]
-        l_page = sb.tile([P, PAGES], F32, name="l_page")
-        w_f32 = [sb.tile([P, PAGE], F32, name=f"w_f32{e}", tag=f"w_f32{e}", align_bytes=64) for e in range(PAGES)]
+        ex_first = sb.tile([P, PAGE], F32, name="ex_first", align_bytes=64)
+        ex_middle = sb.tile([P, 2, PAGE], F32, name="ex_middle", tag="vsc_pool", align_bytes=64)
+        ex_last = sb.tile([P, PAGE], F32, name="ex_last", tag="ex_last", align_bytes=64)
+        ex = [ex_first[:], ex_middle[:, 0], ex_middle[:, 1], ex_last[:]]
+        l_part = sb.tile([P, PAGES + 1], F32, name="l_part")
         th_max = sb.tile([P, 1], F32, name="th_max")
         exp_neg_m = sb.tile([P, 1], F32, name="exp_neg_m")
 
         scores = []
         for e in range(PAGES):
-            nc.vector.tensor_copy(k_g[e][:], k_pool[:].bitcast(U32).indirect(page_offsets(e)))
+            nc.vector.tensor_copy(k_g[:, e * PAGE : (e + 1) * PAGE], k_pool[:].bitcast(U32).indirect(page_offsets(e)))
             width = PAGE // 2 if e == 0 else PAGE
             parts = []
             for c in range(0, PAGE, width):
-                score = ps.tile([P, width], F32, name=f"score{e}_{c}", tag=f"bank{e}" if c == 0 else "spread0")
+                score = ps.tile([P, width], F32, name=f"score{e}_{c}", tag=f"score{e}" if c == 0 else "score0b")
                 nc.tensor.matmul_mx(
                     out=score[:],
                     lhsT=q_codes[:].bitcast(FP8X4),
                     lhsT_scale=q_scales[:],
-                    rhs=k_g[e][:, c : c + width].bitcast(FP8X4),
+                    rhs=k_g[:, e * PAGE + c : e * PAGE + c + width].bitcast(FP8X4),
                     rhs_scale=ks_plane[e // 2][:].bitcast(U8)[:, e % 2 * PAGE + c : e % 2 * PAGE + c + width],
                     start=True,
                     stop=True,
@@ -138,22 +153,24 @@ def tile_attend_pkv8_cap_kernel(tc, qT, k_words, k_scales, v_words, v_scales, vs
                 nc.scalar.activation(th[e][:, c : c + width], score[:], ACT.Tanh, scale=1.0 / CAP)
 
         def exponentiate(e):
-            nc.scalar.activation(ex[e][:], th[e], ACT.Exp, scale=CAP, accum_out=l_page[:, e : e + 1])
+            for c, width, score in scores[e]:
+                col = e if c == 0 else PAGES
+                nc.scalar.activation(
+                    ex[e][:, c : c + width], th[e][:, c : c + width], ACT.Exp, scale=CAP,
+                    accum_out=l_part[:, col : col + 1],
+                )
 
-        def weigh(e):
-            nc.vector.tensor_tensor(w_f32[e][:], vs_pool[:].indirect(page_offsets(e)), ex[e][:], ALU.mult)
-
-        for e in range(last):
-            cap(e)
+        cap(0)
         exponentiate(0)
-        cap(last)
+        for e in range(1, PAGES):
+            cap(e)
+        for e in range(1, last):
+            vs_rows.append(spread(e, f"score{e + 1}"))
         for e in range(last):
-            nc.vector.tensor_reduce(th_all[:, N + e : N + e + 1], th[e], mybir.AxisListType.X, ALU.max)
-        weigh(0)
-        nc.vector.tensor_reduce(th_max[:], th_all[:, last * PAGE :], mybir.AxisListType.X, ALU.max)
+            nc.vector.tensor_reduce(th[last][:, PAGE + e : PAGE + e + 1], th[e][:], mybir.AxisListType.X, ALU.max)
+        nc.vector.tensor_reduce(th_max[:], th[last][:], mybir.AxisListType.X, ALU.max)
         for e in range(1, last):
             exponentiate(e)
-            weigh(e)
         nc.scalar.activation(exp_neg_m[:], th_max[:], ACT.Exp, scale=-CAP)
         exponentiate(last)
 
@@ -165,20 +182,17 @@ def tile_attend_pkv8_cap_kernel(tc, qT, k_words, k_scales, v_words, v_scales, vs
         def by_pairs(row):
             return row.rearrange("q (p u j) -> q u p j", u=2, j=2)
 
-        nc.vector.tensor_scalar(w_row[0][:], by_pairs(w_f32[0][:]), exp_neg_m[:], None, ALU.mult)
-        for e in range(1, last):
-            nc.scalar.activation(w_row[e][:], by_pairs(w_f32[e][:]), ACT.Copy, scale=exp_neg_m[:])
-        for h in range(2):
-            slots = slice(h * PAGE // 2, (h + 1) * PAGE // 2)
-            offsets = offs_sb[:, (last * PAGE + slots.start) // 16 : (last * PAGE + slots.stop) // 16]
-            nc.vector.tensor_tensor(w_f32[last][:, slots], vs_pool[:].indirect(offsets), ex[last][:, slots], ALU.mult)
-        for h in range(2):
-            words = slice(h * P // 2, (h + 1) * P // 2)
-            nc.vector.tensor_scalar(
-                w_row[last][:, :, words, :], by_pairs(w_f32[last][:])[:, :, words, :], exp_neg_m[:], None, ALU.mult
-            )
+        w_first = sb.tile([P, PAGE], F32, name="w_first", tag="th1", align_bytes=64)
+        nc.vector.tensor_tensor(w_first[:], ex[0], vs_rows[0], ALU.mult)
+        vs_rows.append(spread(last, "early"))
+        nc.scalar.activation(w_row[0][:], by_pairs(w_first[:]), ACT.Copy, scale=exp_neg_m[:])
+        for e in range(1, PAGES):
+            for u in range(2):
+                nc.vector.scalar_tensor_tensor(
+                    w_row[e][:, u], by_pairs(ex[e])[:, u], exp_neg_m[:], by_pairs(vs_rows[e])[:, u], ALU.mult, ALU.mult
+                )
         v_g = [
-            sb.tile([P, 2 * DV], U32, name=f"v_g{h}", tag=(f"ex{last}", "w_bf0")[h], align_bytes=64) for h in range(2)
+            sb.tile([P, 2 * DV], U32, name=f"v_g{h}", tag=("ex_last", "w_bf1")[h], align_bytes=64) for h in range(2)
         ]
 
         def gather_values(h):
@@ -188,9 +202,9 @@ def tile_attend_pkv8_cap_kernel(tc, qT, k_words, k_scales, v_words, v_scales, vs
 
         gather_values(0)
 
-        order = (0, 1, 2, 3)
+        order = (1, 0, 2, 3)
         for e in order:
-            turned = ps.tile([P, 2, NQ], F32, name=f"turned{e}", tag=f"bank{e % last}")
+            turned = ps.tile([P, 2, NQ], F32, name=f"turned{e}", tag=("score0b", "score0", "score1", "late0")[e])
             for u in range(2):
                 nc.tensor.transpose(
                     turned[:, u, :], w_row[e][:, u].rearrange("q p j -> q (p j)").bitcast(F32), ident[:]
@@ -202,16 +216,16 @@ def tile_attend_pkv8_cap_kernel(tc, qT, k_words, k_scales, v_words, v_scales, vs
             nc.vector.quantize_mx(
                 out=w_codes[e][:].bitcast(FP8X4), scales=w_scales[e][:], in_=w_bf[e][:].rearrange("p q t -> p (q t)")
             )
-            if e == 1:
+            if e == order[1]:
                 gather_values(1)
 
-        l_scaled = sb.tile([P, PAGES], F32, name="l_scaled")
+        l_scaled = sb.tile([P, PAGES + 1], F32, name="l_scaled")
         l_sum = sb.tile([P, 1], F32, name="l_sum")
-        l_inv = sb.tile([P, 1], F32, name="l_inv", tag="w_bf1", align_bytes=64)
-        nc.scalar.activation(l_scaled[:], l_page[:], ACT.Copy, scale=exp_neg_m[:], accum_out=l_sum[:])
+        l_inv = sb.tile([P, 1], F32, name="l_inv", tag="w_bf0", align_bytes=64)
+        nc.scalar.activation(l_scaled[:], l_part[:], ACT.Copy, scale=exp_neg_m[:], accum_out=l_sum[:])
         nc.vector.reciprocal(l_inv[:], l_sum[:])
 
-        acc = ps.tile([P, DV], F32, name="acc", tag=f"bank{last - 1}")
+        acc = ps.tile([P, DV], F32, name="acc", tag="late1")
         for e in order:
             cols = slice(e * DV, (e + 1) * DV)
             nc.tensor.matmul_mx(
@@ -220,8 +234,8 @@ def tile_attend_pkv8_cap_kernel(tc, qT, k_words, k_scales, v_words, v_scales, vs
                 lhsT_scale=w_scales[e][:],
                 rhs=v_g[e // 2][:, e % 2 * DV : (e % 2 + 1) * DV].bitcast(FP8X4),
                 rhs_scale=vsc_plane[:].bitcast(U8)[:, cols],
-                start=(e == 0),
-                stop=(e == PAGES - 1),
+                start=(e == order[0]),
+                stop=(e == order[-1]),
             )
         y = sb.tile([P, DV], F32, name="y")
         nc.scalar.activation(y[:], acc[:], ACT.Copy, scale=l_inv[:])

@@ -45,8 +45,8 @@ def tile_attend_pkv8_cap_kernel(tc, qT, k_words, k_scales, v_words, v_scales, vs
         k_pool = sb.tile([P, T], I32, name="k_pool", align_bytes=64)
         ident = sb.tile([P, P], F32, name="ident")
 
-        nc.vector.memset(ks_pool[:], 0)
         nc.vector.memset(vsc_pool[:], 0)
+        nc.vector.memset(ks_pool[:], 0)
         nc.vector.memset(vs_pool[0:vs_row, :], 0.0)
         for zeroed in (ks_plane[0], ks_plane[1], vsc_plane):
             nc.vector.memset(zeroed[:], 0)
@@ -56,18 +56,16 @@ def tile_attend_pkv8_cap_kernel(tc, qT, k_words, k_scales, v_words, v_scales, vs
             channel_multiplier=1,
         )
 
-        nc.sync.dma_start(offs_sb[:], offs)
-        nc.sync.dma_start(voffs_sb[:], voffs)
-        nc.scalar.dma_start(vs_pool[vs_row:P, :], vs[0:1, :])
         nc.scalar.dma_start(q_raw[:], qT[0].rearrange("(p j) q -> p j q", j=PACK))
+        nc.scalar.dma_start(vs_pool[vs_row:P, :], vs[0:1, :])
+        nc.sync.dma_start(voffs_sb[:], voffs)
         nc.sync.dma_start(
-            k_pool[:], k_words[0].rearrange("p t r -> p (t r)").bitcast(I32), max_dma_last_dim=4096
-        )
-        nc.scalar.dma_start(ks_pool[0:P:8, :], k_scales[0].bitcast(I32))
-        nc.scalar.dma_start(
             vsc_pool[0:P:8, :].rearrange("f (u e) -> f u e", u=POOL_PAGES),
             v_scales.bitcast(I32).rearrange("u f e -> f u e"),
         )
+        nc.sync.dma_start(offs_sb[:], offs)
+        nc.sync.dma_start(ks_pool[0:P:8, :], k_scales[0].bitcast(I32))
+        nc.sync.dma_start(k_pool[:], k_words[0].rearrange("p t r -> p (t r)").bitcast(I32))
 
         q_bf = sb.tile([P, NQ, PACK], BF16, name="q_bf", align_bytes=64)
         q_codes = sb.tile([P, NQ], U32, name="q_codes", align_bytes=64)
@@ -116,13 +114,13 @@ def tile_attend_pkv8_cap_kernel(tc, qT, k_words, k_scales, v_words, v_scales, vs
 
         vs_rows = [spread(0, "early")]
 
-        k_g = sb.tile([P, N], U32, name="k_g", tag="vsc_pool", align_bytes=64)
+        k_g = sb.tile([P, N], U32, name="k_g", tag="k_g", align_bytes=64)
         th = [
             sb.tile([P, PAGE + (last if e == last else 0)], F32, name=f"th{e}", tag=f"th{e}", align_bytes=64)
             for e in range(PAGES)
         ]
         ex_first = sb.tile([P, PAGE], F32, name="ex_first", align_bytes=64)
-        ex_middle = sb.tile([P, 2, PAGE], F32, name="ex_middle", tag="vsc_pool", align_bytes=64)
+        ex_middle = sb.tile([P, 2, PAGE], F32, name="ex_middle", tag="k_g", align_bytes=64)
         ex_last = sb.tile([P, PAGE], F32, name="ex_last", tag="ex_last", align_bytes=64)
         ex = [ex_first[:], ex_middle[:, 0], ex_middle[:, 1], ex_last[:]]
         l_part = sb.tile([P, PAGES + 1], F32, name="l_part")

@@ -38,8 +38,8 @@ def tile_attend_pkv8_cap_kernel(tc, qT, k_words, k_scales, v_words, v_scales, vs
         voffs_sb = sb.tile([P, PAGES * DV // 16], U16, name="voffs_sb")
         ks_pool = sb.tile([P, T // 4], I32, name="ks_pool", tag="ks_pool", align_bytes=64)
         vsc_pool = sb.tile([P, POOL_PAGES * DV // 4], I32, name="vsc_pool", tag="vsc_pool", align_bytes=64)
-        ks_plane = [sb.tile([P, half // 4], I32, name=f"ks_plane{h}", align_bytes=64) for h in range(2)]
-        vsc_plane = sb.tile([P, PAGES * DV // 4], I32, name="vsc_plane", align_bytes=64)
+        ks_plane = [sb.tile([P, half // 4], I32, name=f"ks_plane{h}", align_bytes=64)[:] for h in range(2)]
+        vsc_plane = sb.tile([P, PAGES * DV // 4], I32, name="vsc_plane", align_bytes=64)[:]
         q_raw = sb.tile([P, PACK, NQ], F32, name="q_raw")
         vs_pool = sb.tile([P, T], F32, name="vs_pool", align_bytes=64)
         k_pool = sb.tile([P, T], I32, name="k_pool", align_bytes=64)
@@ -49,7 +49,7 @@ def tile_attend_pkv8_cap_kernel(tc, qT, k_words, k_scales, v_words, v_scales, vs
         nc.vector.memset(ks_pool[:], 0)
         nc.vector.memset(vs_pool[0:vs_row, :], 0.0)
         for zeroed in (ks_plane[0], ks_plane[1], vsc_plane):
-            nc.vector.memset(zeroed[:], 0)
+            nc.vector.memset(zeroed, 0)
         nc.gpsimd.memset(ident[:], 0.0)
         nc.gpsimd.affine_select(
             out=ident[:], in_=ident[:], compare_op=ALU.not_equal, fill=1.0, base=0, pattern=[[-1, P]],
@@ -95,16 +95,22 @@ def tile_attend_pkv8_cap_kernel(tc, qT, k_words, k_scales, v_words, v_scales, vs
         )
         place_scale_rows(vsc_plane, vsc_g)
 
-        vs_cols = []
-        for e in range(PAGES):
-            vs_g = sb.tile([P, PAGE], F32, name=f"vs_g{e}", align_bytes=64)
-            nc.scalar.activation(vs_g[:], vs_pool[:].indirect(page_offsets(e)), ACT.Copy)
-            upright = ps.tile([P, PACK, P], F32, name=f"upright{e}", tag=("score2", "score1", "score0b", "score0")[e])
+        vs_g = [sb.tile([P, PAGE], F32, name=f"vs_g{e}", align_bytes=64) for e in range(PAGES)]
+        vs_cols = [sb.tile([P, PACK], F32, name=f"vs_cols{e}") for e in range(PAGES)]
+
+        def stand_upright(e, bank):
+            upright = ps.tile([P, PACK, P], F32, name=f"upright{e}", tag=bank)
             for j in range(PACK):
-                nc.tensor.transpose(upright[:, j, :], vs_g[:, j * P : (j + 1) * P], ident[:])
-            cols = sb.tile([P, PACK], F32, name=f"vs_cols{e}")
-            nc.scalar.copy(cols[:], upright[:, :, vs_row])
-            vs_cols.append(cols)
+                nc.tensor.transpose(upright[:, j, :], vs_g[e][:, j * P : (j + 1) * P], ident[:])
+            return upright
+
+        def take_columns(e, upright):
+            nc.scalar.copy(vs_cols[e][:], upright[:, :, vs_row])
+
+        for e in range(PAGES):
+            nc.scalar.activation(vs_g[e][:], vs_pool[:].indirect(page_offsets(e)), ACT.Copy)
+            if e < last:
+                take_columns(e, stand_upright(e, ("score0", "score0b", "score1")[e]))
 
         def spread(e, bank):
             rows = ps.tile([P, PACK, P], F32, name=f"vs_rows{e}", tag=bank)
@@ -114,22 +120,23 @@ def tile_attend_pkv8_cap_kernel(tc, qT, k_words, k_scales, v_words, v_scales, vs
 
         vs_rows = [spread(0, "early")]
 
-        k_g = sb.tile([P, N], U32, name="k_g", tag="k_g", align_bytes=64)
-        th = [
-            sb.tile([P, PAGE + (last if e == last else 0)], F32, name=f"th{e}", tag=f"th{e}", align_bytes=64)
-            for e in range(PAGES)
+        k_g = [sb.tile([P, PAGE], U32, name=f"k_g{e}", tag=f"k_g{e}", align_bytes=64) for e in range(PAGES)]
+        th = [sb.tile([P, PAGE], F32, name=f"th{e}", tag=f"th{e}", align_bytes=64)[:] for e in range(last)]
+        th_tail = sb.tile([P, 2 * PAGE], F32, name="th_tail", align_bytes=64)
+        th.append(th_tail[:, :PAGE])
+        ex = [
+            sb.tile([P, PAGE], F32, name="ex0", align_bytes=64)[:],
+            sb.tile([P, PAGE], F32, name="ex1", tag=f"k_g{last}", align_bytes=64)[:],
+            th_tail[:, PAGE:],
+            sb.tile([P, PAGE], F32, name="ex_last", tag="ex_last", align_bytes=64)[:],
         ]
-        ex_first = sb.tile([P, PAGE], F32, name="ex_first", align_bytes=64)
-        ex_middle = sb.tile([P, 2, PAGE], F32, name="ex_middle", tag="k_g", align_bytes=64)
-        ex_last = sb.tile([P, PAGE], F32, name="ex_last", tag="ex_last", align_bytes=64)
-        ex = [ex_first[:], ex_middle[:, 0], ex_middle[:, 1], ex_last[:]]
         l_part = sb.tile([P, PAGES + 1], F32, name="l_part")
         th_max = sb.tile([P, 1], F32, name="th_max")
         exp_neg_m = sb.tile([P, 1], F32, name="exp_neg_m")
 
         scores = []
         for e in range(PAGES):
-            nc.vector.tensor_copy(k_g[:, e * PAGE : (e + 1) * PAGE], k_pool[:].bitcast(U32).indirect(page_offsets(e)))
+            nc.vector.tensor_copy(k_g[e][:], k_pool[:].bitcast(U32).indirect(page_offsets(e)))
             width = PAGE // 2 if e == 0 else PAGE
             parts = []
             for c in range(0, PAGE, width):
@@ -138,8 +145,8 @@ def tile_attend_pkv8_cap_kernel(tc, qT, k_words, k_scales, v_words, v_scales, vs
                     out=score[:],
                     lhsT=q_codes[:].bitcast(FP8X4),
                     lhsT_scale=q_scales[:],
-                    rhs=k_g[:, e * PAGE + c : e * PAGE + c + width].bitcast(FP8X4),
-                    rhs_scale=ks_plane[e // 2][:].bitcast(U8)[:, e % 2 * PAGE + c : e % 2 * PAGE + c + width],
+                    rhs=k_g[e][:, c : c + width].bitcast(FP8X4),
+                    rhs_scale=ks_plane[e // 2].bitcast(U8)[:, e % 2 * PAGE + c : e % 2 * PAGE + c + width],
                     start=True,
                     stop=True,
                 )
@@ -162,15 +169,17 @@ def tile_attend_pkv8_cap_kernel(tc, qT, k_words, k_scales, v_words, v_scales, vs
         exponentiate(0)
         for e in range(1, PAGES):
             cap(e)
-        for e in range(1, last):
-            vs_rows.append(spread(e, f"score{e + 1}"))
+        upright_last = stand_upright(last, "score2")
+        vs_rows.append(spread(1, "score3"))
         for e in range(last):
-            nc.vector.tensor_reduce(th[last][:, PAGE + e : PAGE + e + 1], th[e][:], mybir.AxisListType.X, ALU.max)
-        nc.vector.tensor_reduce(th_max[:], th[last][:], mybir.AxisListType.X, ALU.max)
-        for e in range(1, last):
-            exponentiate(e)
+            nc.vector.tensor_reduce(th_tail[:, PAGE + e : PAGE + e + 1], th[e], mybir.AxisListType.X, ALU.max)
+        nc.vector.tensor_reduce(th_max[:], th_tail[:, : PAGE + last], mybir.AxisListType.X, ALU.max)
+        exponentiate(1)
+        take_columns(last, upright_last)
+        vs_rows.append(spread(2, "score2"))
         nc.scalar.activation(exp_neg_m[:], th_max[:], ACT.Exp, scale=-CAP)
-        exponentiate(last)
+        for e in range(2, PAGES):
+            exponentiate(e)
 
         w_row = [sb.tile([P, 2, P, 2], BF16, name=f"w_row{e}", align_bytes=64) for e in range(PAGES)]
         w_bf = [sb.tile([P, NQ, PACK], BF16, name=f"w_bf{e}", tag=f"w_bf{e}", align_bytes=64) for e in range(PAGES)]
@@ -231,7 +240,7 @@ def tile_attend_pkv8_cap_kernel(tc, qT, k_words, k_scales, v_words, v_scales, vs
                 lhsT=w_codes[e][:].bitcast(FP8X4),
                 lhsT_scale=w_scales[e][:],
                 rhs=v_g[e // 2][:, e % 2 * DV : (e % 2 + 1) * DV].bitcast(FP8X4),
-                rhs_scale=vsc_plane[:].bitcast(U8)[:, cols],
+                rhs_scale=vsc_plane.bitcast(U8)[:, cols],
                 start=(e == order[0]),
                 stop=(e == order[-1]),
             )

@@ -136,10 +136,11 @@ def tile_attend_pkv8_cap_kernel(tc, qT, k_words, k_scales, v_words, v_scales, vs
 
         scores = []
         for e in range(PAGES):
-            nc.vector.tensor_copy(k_g[e][:], k_pool[:].bitcast(U32).indirect(page_offsets(e)))
             width = PAGE // 2 if e == 0 else PAGE
             parts = []
             for c in range(0, PAGE, width):
+                offsets = page_offsets(e)[:, c // 16 : (c + width) // 16]
+                nc.vector.tensor_copy(k_g[e][:, c : c + width], k_pool[:].bitcast(U32).indirect(offsets))
                 score = ps.tile([P, width], F32, name=f"score{e}_{c}", tag=f"score{e}" if c == 0 else "score0b")
                 nc.tensor.matmul_mx(
                     out=score[:],
@@ -189,10 +190,13 @@ def tile_attend_pkv8_cap_kernel(tc, qT, k_words, k_scales, v_words, v_scales, vs
         def by_pairs(row):
             return row.rearrange("q (p u j) -> q u p j", u=2, j=2)
 
-        w_first = sb.tile([P, PAGE], F32, name="w_first", tag="th1", align_bytes=64)
-        nc.vector.tensor_tensor(w_first[:], ex[0], vs_rows[0], ALU.mult)
+        w_first = sb.tile([P, 2, P, 2], F32, name="w_first", tag="th1", align_bytes=64)
+        nc.vector.tensor_tensor(w_first[:], by_pairs(ex[0]), by_pairs(vs_rows[0]), ALU.mult)
         vs_rows.append(spread(last, "early"))
-        nc.scalar.activation(w_row[0][:], by_pairs(w_first[:]), ACT.Copy, scale=exp_neg_m[:])
+        nc.gpsimd.tensor_scalar(
+            w_row[0][:].rearrange("q u p j -> q (u p j)"), w_first[:].rearrange("q u p j -> q (u p j)"),
+            exp_neg_m[:], 1.0, ALU.mult, ALU.mult,
+        )
         for e in range(1, PAGES):
             for u in range(2):
                 nc.vector.scalar_tensor_tensor(
@@ -228,7 +232,7 @@ def tile_attend_pkv8_cap_kernel(tc, qT, k_words, k_scales, v_words, v_scales, vs
 
         l_scaled = sb.tile([P, PAGES + 1], F32, name="l_scaled")
         l_sum = sb.tile([P, 1], F32, name="l_sum")
-        l_inv = sb.tile([P, 1], F32, name="l_inv", tag="w_bf0", align_bytes=64)
+        l_inv = sb.tile([P, 1], F32, name="l_inv", tag=f"w_bf{last}", align_bytes=64)
         nc.scalar.activation(l_scaled[:], l_part[:], ACT.Copy, scale=exp_neg_m[:], accum_out=l_sum[:])
         nc.vector.reciprocal(l_inv[:], l_sum[:])
 

from contextlib import ExitStack

import concourse.mybir as mybir

N, T, D, DV, NQ = 2048, 4096, 512, 128, 128
PAGE = 512
CAP = 2.0

FLOPS = 2 * NQ * N * (D + DV)
BYTES = D * NQ * 4 + D * T + 16 * T + T * DV + T // 32 * DV + T * 4 + 128 * (N + N // 4) // 16 * 2 + NQ * DV * 4

F32 = mybir.dt.float32
BF16 = mybir.dt.bfloat16
I32 = mybir.dt.int32
U32 = mybir.dt.uint32
U16 = mybir.dt.uint16
U8 = mybir.dt.uint8
FP8X4 = mybir.dt.float8_e4m3fn_x4
ALU = mybir.AluOpType
ACT = mybir.ActivationFunctionType

P = 128
PACK = 4
PAGES = N // PAGE
POOL_PAGES = T // PAGE


def tile_attend_pkv8_cap_kernel(tc, qT, k_words, k_scales, v_words, v_scales, vs, offs, voffs, out):
    nc = tc.nc
    with ExitStack() as ctx:
        sb = ctx.enter_context(tc.tile_pool(name="sb", bufs=1))
        ps = ctx.enter_context(tc.psum_pool(name="ps", bufs=1))

        half = N // 2
        last = PAGES - 1
        vs_row = P - 1
        offs_sb = sb.tile([P, N // 16], U16, name="offs_sb")
        voffs_sb = sb.tile([P, PAGES * DV // 16], U16, name="voffs_sb")
        ks_pool = sb.tile([P, T // 4], I32, name="ks_pool", tag="ks_pool", align_bytes=64)
        vsc_pool = sb.tile([P, POOL_PAGES * DV // 4], I32, name="vsc_pool", tag="vsc_pool", align_bytes=64)
        ks_plane = [sb.tile([P, half // 4], I32, name=f"ks_plane{h}", align_bytes=64)[:] for h in range(2)]
        vsc_plane = sb.tile([P, PAGES * DV // 4], I32, name="vsc_plane", align_bytes=64)[:]
        q_raw = sb.tile([P, PACK, NQ], F32, name="q_raw")
        vs_pool = sb.tile([P, T], F32, name="vs_pool", align_bytes=64)
        k_pool = sb.tile([P, T], I32, name="k_pool", align_bytes=64)
        ident = sb.tile([P, P], F32, name="ident")

        nc.vector.memset(vsc_pool[:], 0)
        nc.vector.memset(ks_pool[:], 0)
        nc.vector.memset(vs_pool[0:vs_row, :], 0.0)
        for zeroed in (ks_plane[0], ks_plane[1], vsc_plane):
            nc.vector.memset(zeroed, 0)
        nc.gpsimd.memset(ident[:], 0.0)
        nc.gpsimd.affine_select(
            out=ident[:], in_=ident[:], compare_op=ALU.not_equal, fill=1.0, base=0, pattern=[[-1, P]],
            channel_multiplier=1,
        )

        nc.scalar.dma_start(q_raw[:], qT[0].rearrange("(p j) q -> p j q", j=PACK))
        nc.scalar.dma_start(vs_pool[vs_row:P, :], vs[0:1, :])
        nc.sync.dma_start(voffs_sb[:], voffs)
        nc.sync.dma_start(
            vsc_pool[0:P:8, :].rearrange("f (u e) -> f u e", u=POOL_PAGES),
            v_scales.bitcast(I32).rearrange("u f e -> f u e"),
        )
        nc.sync.dma_start(offs_sb[:], offs)
        nc.sync.dma_start(ks_pool[0:P:8, :], k_scales[0].bitcast(I32))
        nc.sync.dma_start(k_pool[:], k_words[0].rearrange("p t r -> p (t r)").bitcast(I32))

        q_bf = sb.tile([P, NQ, PACK], BF16, name="q_bf", align_bytes=64)
        q_codes = sb.tile([P, NQ], U32, name="q_codes", align_bytes=64)
        q_scales = sb.tile([P, NQ], U8, name="q_scales", align_bytes=64)
        nc.scalar.activation(q_bf[:], q_raw[:].rearrange("p j q -> p q j"), ACT.Copy)

        def place_scale_rows(plane, gathered):
            for g in range(4):
                nc.sync.dma_start(plane[g:P:32, :], gathered[8 * g : P : 32, :].bitcast(I32))

        def page_offsets(e):
            return offs_sb[:, e * PAGE // 16 : (e + 1) * PAGE // 16]

        for h in range(2):
            ks_g = sb.tile([P, half], U8, name=f"ks_g{h}", align_bytes=64)
            nc.vector.tensor_copy(
                ks_g[:], ks_pool[:].bitcast(U8).indirect(offs_sb[:, h * half // 16 : (h + 1) * half // 16])
            )
            place_scale_rows(ks_plane[h], ks_g)
        nc.vector.quantize_mx(out=q_codes[:].bitcast(FP8X4), scales=q_scales[:], in_=q_bf[:].rearrange("p q j -> p (q j)"))
        vsc_g = sb.tile([P, PAGES * DV], U8, name="vsc_g", align_bytes=64)
        nc.vector.tensor_copy(vsc_g[:], vsc_pool[:].bitcast(U8).indirect(voffs_sb[:]))
        v_pool = sb.tile([P, POOL_PAGES * DV], I32, name="v_pool", tag="ks_pool", align_bytes=64)
        nc.sync.dma_start(
            v_pool[:].rearrange("p (u e) -> p u e", u=POOL_PAGES),
            v_words.rearrange("u p e r -> p u (e r)").bitcast(I32),
        )
        place_scale_rows(vsc_plane, vsc_g)

        vs_g = [sb.tile([P, PAGE], F32, name=f"vs_g{e}", align_bytes=64) for e in range(PAGES)]
        vs_cols = [sb.tile([P, PACK], F32, name=f"vs_cols{e}") for e in range(PAGES)]

        def stand_upright(e, bank):
            upright = ps.tile([P, PACK, P], F32, name=f"upright{e}", tag=bank)
            for j in range(PACK):
                nc.tensor.transpose(upright[:, j, :], vs_g[e][:, j * P : (j + 1) * P], ident[:])
            return upright

        def take_columns(e, upright):
            nc.scalar.copy(vs_cols[e][:], upright[:, :, vs_row])

        for e in range(PAGES):
            nc.scalar.activation(vs_g[e][:], vs_pool[:].indirect(page_offsets(e)), ACT.Copy)
            if e < last:
                take_columns(e, stand_upright(e, ("score0", "score0b", "score1")[e]))

        def spread(e, bank):
            rows = ps.tile([P, PACK, P], F32, name=f"vs_rows{e}", tag=bank)
            for j in range(PACK):
                nc.tensor.transpose(rows[:, j, :], vs_cols[e][:, j : j + 1].to_broadcast([P, P]), ident[:])
            return rows[:].rearrange("q j p -> q (j p)")

        vs_rows = [spread(0, "early")]

        k_g = [sb.tile([P, PAGE], U32, name=f"k_g{e}", tag=f"k_g{e}", align_bytes=64) for e in range(PAGES)]
        th = [sb.tile([P, PAGE], F32, name=f"th{e}", tag=f"th{e}", align_bytes=64)[:] for e in range(last)]
        th_tail = sb.tile([P, 2 * PAGE], F32, name="th_tail", align_bytes=64)
        th.append(th_tail[:, :PAGE])
        ex = [
            sb.tile([P, PAGE], F32, name="ex0", align_bytes=64)[:],
            sb.tile([P, PAGE], F32, name="ex1", tag=f"k_g{last}", align_bytes=64)[:],
            th_tail[:, PAGE:],
            sb.tile([P, PAGE], F32, name="ex_last", tag="ex_last", align_bytes=64)[:],
        ]
        l_part = sb.tile([P, PAGES + 1], F32, name="l_part")
        th_max = sb.tile([P, 1], F32, name="th_max")
        exp_neg_m = sb.tile([P, 1], F32, name="exp_neg_m")

        scores = []
        for e in range(PAGES):
            width = PAGE // 2 if e == 0 else PAGE
            parts = []
            for c in range(0, PAGE, width):
                offsets = page_offsets(e)[:, c // 16 : (c + width) // 16]
                nc.vector.tensor_copy(k_g[e][:, c : c + width], k_pool[:].bitcast(U32).indirect(offsets))
                score = ps.tile([P, width], F32, name=f"score{e}_{c}", tag=f"score{e}" if c == 0 else "score0b")
                nc.tensor.matmul_mx(
                    out=score[:],
                    lhsT=q_codes[:].bitcast(FP8X4),
                    lhsT_scale=q_scales[:],
                    rhs=k_g[e][:, c : c + width].bitcast(FP8X4),
                    rhs_scale=ks_plane[e // 2].bitcast(U8)[:, e % 2 * PAGE + c : e % 2 * PAGE + c + width],
                    start=True,
                    stop=True,
                )
                parts.append((c, width, score))
            scores.append(parts)

        def cap(e):
            for c, width, score in scores[e]:
                nc.scalar.activation(th[e][:, c : c + width], score[:], ACT.Tanh, scale=1.0 / CAP)

        def exponentiate(e):
            for c, width, score in scores[e]:
                col = e if c == 0 else PAGES
                nc.scalar.activation(
                    ex[e][:, c : c + width], th[e][:, c : c + width], ACT.Exp, scale=CAP,
                    accum_out=l_part[:, col : col + 1],
                )

        cap(0)
        exponentiate(0)
        for e in range(1, PAGES):
            cap(e)
        upright_last = stand_upright(last, "score2")
        vs_rows.append(spread(1, "score3"))
        for e in range(last):
            nc.vector.tensor_reduce(th_tail[:, PAGE + e : PAGE + e + 1], th[e], mybir.AxisListType.X, ALU.max)
        nc.vector.tensor_reduce(th_max[:], th_tail[:, : PAGE + last], mybir.AxisListType.X, ALU.max)
        exponentiate(1)
        take_columns(last, upright_last)
        vs_rows.append(spread(2, "score2"))
        nc.scalar.activation(exp_neg_m[:], th_max[:], ACT.Exp, scale=-CAP)
        for e in range(2, PAGES):
            exponentiate(e)

        w_row = [sb.tile([P, 2, P, 2], BF16, name=f"w_row{e}", align_bytes=64) for e in range(PAGES)]
        w_bf = [sb.tile([P, NQ, PACK], BF16, name=f"w_bf{e}", tag=f"w_bf{e}", align_bytes=64) for e in range(PAGES)]
        w_codes = [sb.tile([P, NQ], U32, name=f"w_codes{e}", align_bytes=64) for e in range(PAGES)]
        w_scales = [sb.tile([P, NQ], U8, name=f"w_scales{e}", align_bytes=64) for e in range(PAGES)]

        def by_pairs(row):
            return row.rearrange("q (p u j) -> q u p j", u=2, j=2)

        w_first = sb.tile([P, 2, P, 2], F32, name="w_first", tag="th1", align_bytes=64)
        nc.vector.tensor_tensor(w_first[:], by_pairs(ex[0]), by_pairs(vs_rows[0]), ALU.mult)
        vs_rows.append(spread(last, "early"))
        nc.gpsimd.tensor_scalar(
            w_row[0][:].rearrange("q u p j -> q (u p j)"), w_first[:].rearrange("q u p j -> q (u p j)"),
            exp_neg_m[:], 1.0, ALU.mult, ALU.mult,
        )
        for e in range(1, PAGES):
            for u in range(2):
                nc.vector.scalar_tensor_tensor(
                    w_row[e][:, u], by_pairs(ex[e])[:, u], exp_neg_m[:], by_pairs(vs_rows[e])[:, u], ALU.mult, ALU.mult
                )
        v_g = [
            sb.tile([P, 2 * DV], U32, name=f"v_g{h}", tag=("ex_last", "w_bf1")[h], align_bytes=64) for h in range(2)
        ]

        def gather_values(h):
            nc.vector.tensor_copy(
                v_g[h][:], v_pool[:].bitcast(U32).indirect(voffs_sb[:, h * 2 * DV // 16 : (h + 1) * 2 * DV // 16])
            )

        gather_values(0)

        order = (1, 0, 2, 3)
        for e in order:
            turned = ps.tile([P, 2, NQ], F32, name=f"turned{e}", tag=("score0b", "score0", "score1", "late0")[e])
            for u in range(2):
                nc.tensor.transpose(
                    turned[:, u, :], w_row[e][:, u].rearrange("q p j -> q (p j)").bitcast(F32), ident[:]
                )
            nc.scalar.copy(
                w_bf[e][:].rearrange("p q t -> p (q t)").bitcast(F32).rearrange("p (q u) -> p q u", u=2),
                turned[:].rearrange("p u q -> p q u"),
            )
            nc.vector.quantize_mx(
                out=w_codes[e][:].bitcast(FP8X4), scales=w_scales[e][:], in_=w_bf[e][:].rearrange("p q t -> p (q t)")
            )
            if e == order[1]:
                gather_values(1)

        l_scaled = sb.tile([P, PAGES + 1], F32, name="l_scaled")
        l_sum = sb.tile([P, 1], F32, name="l_sum")
        l_inv = sb.tile([P, 1], F32, name="l_inv", tag=f"w_bf{last}", align_bytes=64)
        nc.scalar.activation(l_scaled[:], l_part[:], ACT.Copy, scale=exp_neg_m[:], accum_out=l_sum[:])
        nc.vector.reciprocal(l_inv[:], l_sum[:])

        acc = ps.tile([P, DV], F32, name="acc", tag="late1")
        for e in order:
            cols = slice(e * DV, (e + 1) * DV)
            nc.tensor.matmul_mx(
                out=acc[:],
                lhsT=w_codes[e][:].bitcast(FP8X4),
                lhsT_scale=w_scales[e][:],
                rhs=v_g[e // 2][:, e % 2 * DV : (e % 2 + 1) * DV].bitcast(FP8X4),
                rhs_scale=vsc_plane.bitcast(U8)[:, cols],
                start=(e == order[0]),
                stop=(e == order[-1]),
            )
        y = sb.tile([P, DV], F32, name="y")
        nc.scalar.activation(y[:], acc[:], ACT.Copy, scale=l_inv[:])
        nc.sync.dma_start(out[0], y[:])
